import numpy as np, ml_dtypes
CORES = [1,5,17,21,33,37,49,53]
N = 8
import mx_ref
BF = ml_dtypes.bfloat16
def entries(a):
    return np.ascontiguousarray(a.T).reshape(-1)
def table(e):
    return np.ascontiguousarray(np.reshape(e, (-1, 16)).T).astype(np.int32)
def cols(t, e):
    v = np.concatenate([t.reshape(128, -1, 4), np.zeros((128, 1, 4), BF)], axis=1)
    return np.ascontiguousarray(v[:, e]).reshape(128, -1)
def cut(t, i, w=512):
    return t[:, w * i:w * i + w]
def f(rng, *shape):
    return mx_ref.flush((rng.standard_normal(shape, dtype=np.float32) * np.exp2(rng.integers(-2, 3, shape[:-1] + (1,)))).astype(BF))
def wide(rng, *shape, cols=0):
    v = rng.standard_normal(shape, dtype=np.float32) * np.exp2(rng.integers(-12, 13, shape)).astype(np.float32)
    if cols: v *= np.repeat(np.exp2(rng.integers(-cols, cols + 1, shape[:-2] + (1, shape[-1] // 4))) * (rng.random(shape[:-2] + (1, shape[-1] // 4)) > 0.0625), 4, axis=-1).astype(np.float32)
    return mx_ref.flush(v.astype(BF))
T, O = 384, 1
def places(rng, dest):
    e = np.zeros((N, T), int)
    for d in range(N): e[dest == d] = d * T + rng.permutation(T)
    return np.stack([table(e[r]) for r in range(N)])
def relabel(rng):
    p = rng.permutation(N)
    if np.all((p - np.arange(N)) % N == p[0]): p[[0, 1]] = p[[1, 0]]
    return p
def setup_inputs(rng):
    e = rng.permutation(N * T).reshape(N, T)
    return {"x": f(rng, N, 128, 4 * T), "to": np.stack([table(e[r]) for r in range(N)]), "w": f(rng, N, 128, 512 * O)}
def setup_inputs_swap(rng):
    d = setup_inputs(rng); p = rng.permutation(N); dest = np.zeros((N, T), int)
    for k in range(N): dest[p[k]] = p[(k + 1) % N]
    d["to"] = places(rng, dest); return d
def setup_inputs_ones(rng):
    d = setup_inputs(rng); i = np.arange(N); n = np.ones((N, N), int); n[i, rng.permutation(N)] += T % N
    for t in range(T // N - 1): n[i, rng.permutation(N)] += N
    d["to"] = places(rng, np.stack([rng.permutation(np.repeat(i, n[r])) for r in range(N)])); return d
def setup_inputs_runs(rng):
    d = setup_inputs(rng); p = relabel(rng); s, u = rng.integers(1, N), rng.integers(0, N); g, h = rng.permutation(N), rng.permutation(N)
    n = T // N + ((g[:, None] + h) % N < T % N)
    j = (np.arange(N) + s * np.arange(N)[:, None] + u) % N
    d["to"] = places(rng, np.stack([np.repeat(p[j[r]], n[r, j[r]]) for r in range(N)])); return d
def setup_inputs_comb(rng):
    d = setup_inputs(rng); p = relabel(rng); s, u = rng.integers(1, N), rng.integers(0, N); k = rng.permutation(N); c = np.arange(T)
    d["to"] = places(rng, np.stack([p[(c + np.where(c < T - T % N, s * r + u, k[r])) % N] for r in range(N)])); return d
def setup_inputs_spread(rng):
    d = setup_inputs(rng); d["x"] = wide(rng, N, 128, 4 * T, cols=8); return d
def check_inputs(d):
    e = np.concatenate([entries(d["to"][r]) for r in range(N)])
    return [] if np.array_equal(np.sort(e), np.arange(N * T)) else ["to"]
def reference(x, to, w):
    z = np.concatenate([x[r] for r in range(N)], axis=1)
    e = np.concatenate([entries(to[r]) for r in range(N)])
    home = np.zeros(N * T, int); home[e] = np.arange(N * T)
    y = np.zeros((N, 128, O * T), np.float32)
    for d in range(N):
        v = mx_ref.quantize(cols(z, home[d * T:d * T + T]))
        for o in range(O): y[d][:, T * o:T * o + T] = mx_ref.matmul(mx_ref.quantize(np.ascontiguousarray(cut(w[d], o))), v)
    return {"y": y}

@@ -1,0 +1,421 @@
+from concourse.bass import DstId, RemoteDMATransfer
+from concourse.mybir import dt, AluOpType as A, ActivationFunctionType as AF
+
+T0, N, Q1, CAP, SW = 384, 8, 48, 56, 64
+OWN = 64
+L2 = OWN + 7 * CAP
+H2 = L2 // 2
+PAD = 8192.0
+X4, U8, U16, F32, BF, I32 = "float8_e4m3fn_x4", "uint8", "uint16", "float32", "bfloat16", "int32"
+
+
+def sb(n, t):
+    return ("sbuf", [128] + (list(n) if isinstance(n, (list, tuple)) else [n]), t)
+
+
+SCRATCH = {
+    "xt": sb(1536, BF), "wt": sb(512, BF), "qx": sb(T0, X4), "sx": sb(T0, U8), "qw": sb(128, X4), "sw": sb(128, U8),
+    "slot1c": sb(T0, X4), "slot1s": sb(T0, U8), "land1c": sb(T0, X4), "land1s": sb(T0, U8),
+    "slot2c": sb(512, X4), "slot2s": sb(512, U8), "land2c": sb(L2, X4), "land2s": sb(L2, U8),
+    "tab": sb(24, I32), "key": sb(24, I32), "M": sb(192, F32), "M2": sb(192, F32), "Mm": sb(8, F32), "W": sb(192, F32),
+    "z192": sb(192, F32), "rst": sb(192, F32), "rst32": sb(32, F32), "tabf": sb(32, F32), "trr": sb(32, F32),
+    "torow": sb(512, F32), "tin": sb(32, F32), "tt0": sb(32, F32), "Qs": sb(32, F32), "tb": sb(96, F32),
+    "tb2": sb(96, F32), "F": sb(8, F32), "S": sb(192, F32), "Z": sb(192, F32), "Z1": sb(96, F32), "Z2": sb(48, F32),
+    "P": sb(24, I32), "u1": sb(24, I32), "w1": sb(24, F32), "off1": sb(24, U16), "cval": sb(T0, BF),
+    "win1": sb(768, BF), "tr1": sb(768, BF), "G": sb(24, F32), "g1": sb(24, U16), "ofp": sb(32, U16),
+    "sg": sb(512, F32), "srow": sb(4096, F32),
+    "pidx": sb(4, I32), "pi15": sb(4, I32), "pi16": sb(4, I32), "par128": sb(1, F32), "par16": sb(1, F32),
+    "par1": sb(1, F32), "k16": sb(4, F32), "fl4": sb(4, F32), "kp": sb(4, F32), "kt": sb(4, F32), "kpo": sb(4, F32),
+    "cstA": sb(64, F32), "c4096": sb(8, F32), "clampc": sb(32, F32), "dumpc": sb(32, F32),
+    "st": sb(64, U16), "stf": sb(64, F32), "nn": sb(64, F32), "ci": sb(64, I32), "c8p": sb(128, I32),
+    "e1p": sb(128, F32), "e2p": sb(128, F32), "B": sb(64, F32), "x1": sb(64, F32), "x2": sb(64, F32), "ai": sb(64, I32),
+    "ti": sb(64, I32), "J": sb(64, F32), "cm": sb((4, 64), F32), "pr": sb((4, 64), F32), "t1": sb((4, 32), F32),
+    "t2": sb((4, 16), F32), "t3": sb((4, 8), F32), "off2": sb(32, U16),
+    "y1": sb(8, F32), "y2": sb(8, F32), "a2": sb((8, 8), I32), "ti2": sb((8, 8), I32), "J2": sb((8, 8), F32),
+    "Bx": sb((8, 8), F32), "cm2": sb((32, 8), F32), "pr2": sb((32, 8), F32), "v1": sb((32, 4), F32),
+    "v2": sb((32, 2), F32), "v3": sb((4, 8), F32), "o3a": sb(32, F32), "o3b": sb(32, F32), "off3": sb(32, U16),
+    "sg2": sb(512, F32), "tr3": sb(512, F32), "pt": sb(32, F32), "pg": sb(32, F32), "pu": sb(32, F32), "pl": sb(32, I32),
+    "ph": sb(32, I32), "pw": sb(32, F32), "off4": sb(32, U16), "locA": sb(512, F32), "locF": sb(512, F32),
+    "locO": sb(512, F32), "val": sb(512, BF), "win2": sb(2048, BF), "tr2": sb(768, BF), "G2": sb(24, F32),
+    "off5": sb(24, U16), "ysb": sb(L2, F32), "yo": sb(T0, F32),
+    "sland": ("dram", [8, 128, 4], F32), "ps": ("psum", [128, 1024], F32),
+}
+SEMAPHORES = ["vq", "sq", "gc1", "gc2", "lt", "lx", "lw", "ms", "m2", "trs", "torw", "sto", "qxs", "g1s", "pk1c", "pk1s",
+              "ofps", "own1s", "sgs", "stst", "srz", "wz", "off2s", "pk2c", "pk2s", "own2c", "own2s", "srl", "mm0", "mm1",
+              "cpv", "cps", "off5s", "yv", "ys", "yst", "qws", "sst", "sls", "p1", "p2", "loc"]
+
+
+def plan(topo, ranks, r):
+    me = ranks[r]
+    order = [(r + i) % N for i in range(1, N)]
+    far = [d for d in order if topo.chip(ranks[d]) != topo.chip(me)]
+    near = [d for d in order if topo.chip(ranks[d]) == topo.chip(me)]
+    e = topo.engines(me, ranks[far[0]])
+
+    def m(es):
+        return sum(1 << x for x in es)
+    first = [(d, m(e[2 * i:2 * i + 2])) for i, d in enumerate(far[:4])]
+    second = [(d, m(e[4 * i:4 * i + 4])) for i, d in enumerate(far[4:])]
+    for d in near:
+        first.append((d, m([x for x in topo.engines(me, ranks[d]) if x not in e])))
+    return [first, second]
+
+
+def bits(m):
+    return bin(m).count("1")
+
+
+def rank_program(g, core, T, topo):
+    me = T.rank_of(core)
+    if me is None:
+        return
+    ranks = list(T.cores)
+    V, S, Y, TE, sem = g.vector, g.scalar, g.sync, g.tensor, T.sem
+    vn, ln = [0], [0]
+
+    def v(ins, name=None):
+        if name is None:
+            ins.then_inc(sem.vq, 1)
+            vn[0] += 1
+        else:
+            ins.then_inc(sem[name], 1)
+
+    def vw():
+        V.wait_ge(sem.vq, vn[0])
+
+    def ts(out, in0, s1, s2, o0, o1=None, name=None):
+        v(V.tensor_scalar(out, in0, s1, s2, o0, o1) if o1 is not None else V.tensor_scalar(out, in0, s1, s2, o0), name)
+
+    def tt(out, a, b, op, name=None):
+        v(V.tensor_tensor(out, a, b, op), name)
+
+    def cp(out, in_, name=None):
+        v(V.tensor_copy(out, in_), name)
+
+    def dst(d):
+        a = topo.addr(ranks[d])
+        return DstId(rid=a[0], pnc=a[1])
+
+    def send(group, srcs, dsts, rsem):
+        ts_ = [RemoteDMATransfer(dst_ids=[dst(d)], dma_engine_mask=m, remote_sem=rsem, src=srcs(d), dst=dsts(d))
+               for d, m in group]
+        g.remote_dma_fused(ts_, local_sem=sem.loc)
+        ln[0] += sum(bits(m) for _, m in group)
+
+    def incoming(calls):
+        return calls * sum(bits(m) for r in range(N) if r != me for grp in plan(topo, ranks, r) for d, m in grp if d == me)
+
+    far_d = [d for d in range(N) if topo.chip(ranks[d]) != topo.chip(core)][0]
+    all_mask = topo.mask(core, ranks[far_d])
+    everyone = [(me + i) % N for i in range(1, N)]
+
+    for q in range(8):
+        (Y if q % 2 == 0 else S).dma_start(T.tab[16 * q:16 * q + 16, :], T.to[:]).then_inc(sem.lt, 16)
+    S.dma_start(T.xt[:], T.x[:]).then_inc(sem.lx, 16)
+    Y.dma_start(T.wt[:], T.w[:]).then_inc(sem.lw, 16)
+
+    def iota(out, pat, base, cm, s):
+        (g.iota(out, pat, base, cm) if s[1] else
+         g.iota(out, pat, base, cm, allow_small_or_imprecise_dtypes=True)).then_inc(sem[s[0]], 1)
+    iota(T.pidx[:], [[0, 4]], 0, 1, ("gc1", True))
+    iota(T.cval[:], [[1, T0]], -192, 0, ("gc1", False))
+    c2 = ("gc2", False)
+    iota(T.k16[:], [[16, 4]], 0, 0, c2)
+    iota(T.fl4[:], [[0, 2], [-32, 2]], 16, 0, c2)
+    iota(T.cstA[:], [[T0, 8], [0, 8]], 7 - me, 0, c2)
+    iota(T.c4096[:], [[4096, 8]], 0, 0, c2)
+    iota(T.clampc[:], [[64, 8], [0, 4]], 7 * 512 + 63, 0, c2)
+    iota(T.dumpc[:], [[16, 32]], T0, 1, c2)
+    iota(T.locF[:], [[0, 16], [-32, 2], [0, 16]], 16, 0, c2)
+    ng2 = 7
+    for lo, hi in ((0, me), (me, me + 1), (me + 1, N)):
+        if lo < hi:
+            b = 0 if lo == me else OWN + CAP * ((lo - me - 1) % N)
+            iota(T.locA[:, SW * lo:SW * hi], [[CAP, hi - lo], [1, SW]], b - 200, 0, c2)
+            ng2 += 1
+
+    v(V.memset(T.tabf[:], PAD))
+    v(V.memset(T.tin[:], 0.0))
+    v(V.memset(T.z192[:], 0.0))
+    v(V.memset(T.rst[:], 1.0))
+    v(V.memset(T.rst32[:], 1.0))
+    v(V.memset(T.torow[:], 0.0), "wz")
+    v(V.memset(T.win1[:], 0.0))
+    v(V.memset(T.c8p[:, 0:64], 0))
+    v(V.memset(T.e1p[:, 0:64], 0.0))
+    v(V.memset(T.e2p[:, 0:64], 0.0))
+    v(V.memset(T.ofp[:], T0))
+    vw()
+    v(V.memset(T.rst[:, 0:192:24], 0.0))
+    v(V.memset(T.rst32[:, 0:32:16], 0.0))
+    V.wait_ge(sem.gc1, 2)
+    ts(T.pi15[:], T.pidx[:], 15, None, A.bitwise_and)
+    ts(T.pi16[:], T.pidx[:], 16, None, A.bitwise_and)
+    vw()
+    ts(T.par128[:], T.pi16[:, 0:1], 8.0, None, A.mult)
+    ts(T.par16[:], T.pi16[:, 0:1], 1.0, None, A.mult)
+    ts(T.par1[:], T.pi16[:, 0:1], 0.0625, None, A.mult)
+
+    V.wait_ge(sem.lt, 128)
+    ts(T.key[:], T.tab[:], 1.0 / T0, 0.5 / T0 - 0.5, A.mult, A.add)
+    vw()
+    for d in range(N):
+        ts(T.M[:, 24 * d:24 * d + 24], T.key[:], float(d), None, A.is_equal, None, "ms")
+    cp(T.tabf[:, 0:24], T.tab[:])
+    V.wait_ge(sem.ms, N)
+    v(V.tensor_tensor_scan(T.W[:], T.M[:], T.z192[:], 0.0, A.add, A.add))
+    vw()
+    cp(T.tin[:, 1:9], T.W[:, 23:192:24])
+    v(V.transpose(T.trr[:], T.tabf[:]), "trs")
+    vw()
+    v(V.transpose(T.tt0[:], T.tin[:]))
+    vw()
+    v(V.tensor_tensor_scan(T.Qs[:], T.rst32[:], T.tt0[:], 0.0, A.mult, A.add))
+    vw()
+    tt(T.tb[:, 32:64], T.Qs[:], T.tt0[:], A.subtract)
+    ts(T.tb[:, 64:96], T.Qs[:], 0.0, T.Qs[:, 15:16], A.mult, A.add)
+    vw()
+    ts(T.tb[:, 0:32], T.tb[:, 32:64], -1.0, T.Qs[:, 15:16], A.mult, A.add)
+    vw()
+    v(V.transpose(T.tb2[:], T.tb[:]))
+    vw()
+    tt(T.F[:], T.tb2[:, 0:8], T.tb2[:, 33:41], A.add)
+    cp(T.st[:, 8 * me:8 * me + 8], T.tb2[:, 64:72], "sto")
+    S.wait_ge(sem.ms, N)
+    S.activation(T.M2[:], T.M[:], AF.Copy).then_inc(sem.m2, 1)
+    S.activation(T.Mm[:], T.M[:, 0:192:24], AF.Identity, -1.0).then_inc(sem.m2, 1)
+    V.wait_ge(sem.m2, 2)
+    vw()
+    tt(T.M2[:, 0:192:24], T.Mm[:], T.F[:], A.add)
+    vw()
+    v(V.tensor_tensor_scan(T.S[:], T.rst[:], T.M2[:], 0.0, A.mult, A.add))
+    vw()
+    tt(T.Z[:], T.S[:], T.M[:], A.mult)
+    vw()
+    tt(T.Z1[:], T.Z[:, 0:96], T.Z[:, 96:192], A.add)
+    vw()
+    tt(T.Z2[:], T.Z1[:, 0:48], T.Z1[:, 48:96], A.add)
+    vw()
+    tt(T.P[:], T.Z2[:, 0:24], T.Z2[:, 24:48], A.add)
+    vw()
+    ts(T.u1[:], T.P[:], 384, None, A.bitwise_and)
+    vw()
+    tt(T.w1[:], T.P[:], T.u1[:], A.add)
+    vw()
+    ts(T.off1[:], T.w1[:], T.par128[:], None, A.add)
+    vw()
+    cp(T.win1[:, 0:768].indirect(T.off1[:, 0:24]), T.cval[:])
+    V.wait_ge(sem.lx, 16)
+    v(V.quantize_mx(T.qx[:], T.sx[:], T.xt[:]), "qxs")
+    vw()
+    for m in range(N):
+        v(V.transpose(T.tr1[:, 96 * m:96 * m + 96], T.win1[:, m:768:8]))
+    vw()
+    tt(T.G[:], T.tr1[:, 0:768:32], T.tr1[:, 16:768:32], A.add)
+    vw()
+    ts(T.g1[:], T.G[:], 192.0, None, A.add, None, "g1s")
+    V.wait_ge(sem.g1s, 1)
+    V.wait_ge(sem.qxs, 1)
+    cp(T.slot1c[:].bitcast(dt.uint32), T.qx[:].bitcast(dt.uint32).indirect(T.g1[:, 0:24]), "pk1c")
+    S.wait_ge(sem.g1s, 1)
+    S.wait_ge(sem.qxs, 1)
+    S.activation(T.slot1s[:], T.sx[:].indirect(T.g1[:, 0:24]), AF.Copy).then_inc(sem.pk1s, 1)
+    for h in range(3):
+        ts(T.ofp[:, h:32:4], T.G[:, h:24:3], 192.0, None, A.add, None, "ofps")
+    V.wait_ge(sem.ofps, 3)
+    cp(T.land1c[:, Q1 * me:Q1 * me + Q1].bitcast(dt.uint32),
+       T.qx[:].bitcast(dt.uint32).indirect(T.ofp[:, 4 * me:4 * me + 3]))
+    S.wait_ge(sem.ofps, 3)
+    S.activation(T.land1s[:, Q1 * me:Q1 * me + Q1], T.sx[:].indirect(T.ofp[:, 4 * me:4 * me + 3]), AF.Copy).then_inc(sem.own1s, 1)
+
+    g.wait_ge(sem.sto, 1)
+    g.remote_dma_fused([RemoteDMATransfer(dst_ids=[dst(d) for d in everyone], dma_engine_mask=all_mask, remote_sem=sem.sst,
+                                          srcs=[T.st[:, 8 * me:8 * me + 8]], dsts=[T.st[:, 8 * me:8 * me + 8] for d in everyone])],
+                       local_sem=sem.loc)
+    ln[0] += bits(all_mask)
+    groups = plan(topo, ranks, me)
+    g.wait_ge(sem.pk1c, 1)
+    for i, grp in enumerate(groups):
+        send(grp, lambda d: T.slot1c[:, Q1 * d:Q1 * d + Q1].bitcast(dt.uint8),
+             lambda d: T.land1c[:, Q1 * me:Q1 * me + Q1].bitcast(dt.uint8), sem.p1)
+        if i == 0:
+            g.wait_ge(sem.pk1s, 1)
+        send(grp, lambda d: T.slot1s[:, Q1 * d:Q1 * d + Q1], lambda d: T.land1s[:, Q1 * me:Q1 * me + Q1], sem.p1)
+
+    Y.wait_ge(sem.trs, 1)
+    Y.wait_ge(sem.wz, 1)
+    Y.dma_start(T.torow[0:1, :], T.trr[0:32, 0:16]).then_inc(sem.torw, 16)
+    S.wait_ge(sem.torw, 16)
+    S.wait_ge(sem.wz, 1)
+    S.activation(T.sg[:], T.torow[:].indirect(T.ofp[:]), AF.Copy).then_inc(sem.sgs, 1)
+    Y.wait_ge(sem.sgs, 1)
+    Y.dma_start(T.sland[me], T.sg[0:1, :]).then_inc(sem.stst, 16)
+    g.wait_ge(sem.stst, 16)
+    g.remote_dma_fused([RemoteDMATransfer(dst_ids=[dst(d) for d in everyone], dma_engine_mask=all_mask, remote_sem=sem.sls,
+                                          srcs=[T.sland[me]], dsts=[T.sland[me] for d in everyone])], local_sem=sem.loc)
+    ln[0] += bits(all_mask)
+
+    v(V.memset(T.win2[:], 0.0), "off2s")
+    V.wait_ge(sem.gc2, ng2)
+    ts(T.locO[:], T.locF[:], T.par1[:], None, A.mult)
+    tt(T.kp[:], T.pi15[:], T.k16[:], A.add)
+    ts(T.kt[:], T.fl4[:], T.par1[:], None, A.mult)
+    vw()
+    tt(T.kpo[:], T.kp[:], T.kt[:], A.add)
+    tt(T.val[:], T.locA[:], T.locO[:], A.add)
+    S.wait_ge(sem.off2s, 1)
+    for h in range(2):
+        S.activation(T.srow[:, 2048 * h:2048 * h + 2048], T.win2[:], AF.Copy).then_inc(sem.srz, 1)
+    V.wait_ge(sem.lw, 16)
+    v(V.quantize_mx(T.qw[:], T.sw[:], T.wt[:]), "qws")
+
+    nst = bits(all_mask) * (N - 1)
+    V.wait_ge(sem.sst, nst)
+    V.wait_ge(sem.sto, 1)
+    cp(T.stf[:], T.st[:])
+    vw()
+    tt(T.nn[:, 0:63], T.stf[:, 1:64], T.stf[:, 0:63], A.subtract)
+    vw()
+    ts(T.nn[:, 7:64:8], T.stf[:, 7:64:8], -1.0, float(T0), A.mult, A.add)
+    vw()
+    ts(T.ci[:], T.nn[:], 7.0, None, A.add)
+    vw()
+    ts(T.c8p[:, 64:128], T.ci[:], 3, None, A.arith_shift_right)
+    vw()
+    tt(T.e1p[:, 64:128], T.c8p[:, 56:120], T.c8p[:, 48:112], A.add)
+    vw()
+    tt(T.e2p[:, 64:128], T.e1p[:, 64:128], T.e1p[:, 48:112], A.add)
+    vw()
+    tt(T.B[:], T.e2p[:, 64:128], T.e2p[:, 32:96], A.add)
+    tt(T.x2[:], T.cstA[:], T.stf[:], A.add)
+    tt(T.y2[:], T.c4096[:], T.stf[:, me:64:8], A.add)
+    vw()
+    ts(T.x1[:], T.B[:], -8.0, None, A.mult)
+    vw()
+    tt(T.ai[:], T.x1[:], T.x2[:], A.add)
+    for kk in range(4):
+        ts(T.cm[:, kk, :], T.B[:], T.kp[:, kk:kk + 1], None, A.is_le)
+    vw()
+    ts(T.ti[:], T.ai[:], 3, None, A.arith_shift_right)
+    tt(T.y1[:], T.x1[:, me:64:8], T.y2[:], A.add)
+    vw()
+    tt(T.J[:, 8:64], T.ti[:, 8:64], T.ti[:, 0:56], A.subtract)
+    cp(T.J[:, 0:8], T.ti[:, 0:8])
+    vw()
+    for kk in range(4):
+        tt(T.pr[:, kk, :], T.cm[:, kk, :], T.J[:], A.mult)
+    vw()
+    tt(T.t1[:], T.pr[:, :, 0:32], T.pr[:, :, 32:64], A.add)
+    vw()
+    tt(T.t2[:], T.t1[:, :, 0:16], T.t1[:, :, 16:32], A.add)
+    vw()
+    tt(T.t3[:], T.t2[:, :, 0:8], T.t2[:, :, 8:16], A.add)
+    vw()
+    for kk in range(4):
+        ts(T.off2[:, kk:32:4], T.t3[:, kk, :], T.kp[:, kk:kk + 1], float(T0 - 1), A.add, A.min, "off2s")
+    for m in range(N):
+        ts(T.a2[:, m, :], T.y1[:], float(7 - m + 512 * m), None, A.add)
+        cp(T.Bx[:, m, :], T.B[:, me:64:8])
+    vw()
+    ts(T.ti2[:], T.a2[:], 3, None, A.arith_shift_right)
+    for kk in range(4):
+        ts(T.cm2[:, 8 * kk:8 * kk + 8, :], T.Bx[:], T.kpo[:, kk:kk + 1], None, A.is_le)
+    vw()
+    tt(T.J2[:, :, 1:8], T.ti2[:, :, 1:8], T.ti2[:, :, 0:7], A.subtract)
+    cp(T.J2[:, :, 0:1], T.ti2[:, :, 0:1])
+    vw()
+    for kk in range(4):
+        tt(T.pr2[:, 8 * kk:8 * kk + 8, :], T.cm2[:, 8 * kk:8 * kk + 8, :], T.J2[:], A.mult)
+    vw()
+    tt(T.v1[:], T.pr2[:, :, 0:4], T.pr2[:, :, 4:8], A.add)
+    vw()
+    tt(T.v2[:], T.v1[:, :, 0:2], T.v1[:, :, 2:4], A.add)
+    vw()
+    for kk in range(4):
+        tt(T.v3[:, kk, :], T.v2[:, 8 * kk:8 * kk + 8, 0], T.v2[:, 8 * kk:8 * kk + 8, 1], A.add)
+    vw()
+    for kk in range(4):
+        ts(T.o3a[:, kk:32:4], T.v3[:, kk, :], T.kpo[:, kk:kk + 1], None, A.add)
+    vw()
+    tt(T.o3b[:], T.o3a[:], T.clampc[:], A.min)
+    vw()
+    cp(T.off3[:], T.o3b[:])
+
+    V.wait_ge(sem.off2s, 5)
+    V.wait_ge(sem.p1, incoming(2))
+    vw()
+    cp(T.slot2c[:].bitcast(dt.uint32), T.land1c[:].bitcast(dt.uint32).indirect(T.off2[:]), "pk2c")
+    cp(T.land2c[:, 0:OWN].bitcast(dt.uint32), T.land1c[:].bitcast(dt.uint32).indirect(T.off2[:, 4 * me:4 * me + 4]), "own2c")
+    S.wait_ge(sem.off2s, 5)
+    S.wait_ge(sem.p1, incoming(2))
+    S.wait_ge(sem.own1s, 1)
+    S.activation(T.slot2s[:], T.land1s[:].indirect(T.off2[:]), AF.Copy).then_inc(sem.pk2s, 1)
+    S.activation(T.land2s[:, 0:OWN], T.land1s[:].indirect(T.off2[:, 4 * me:4 * me + 4]), AF.Copy).then_inc(sem.own2s, 1)
+
+    def blk(d):
+        a = OWN + CAP * ((me - d - 1) % N)
+        return slice(a, a + CAP)
+    g.wait_ge(sem.pk2c, 1)
+    for i, grp in enumerate(groups):
+        send(grp, lambda d: T.slot2c[:, SW * d:SW * d + CAP].bitcast(dt.uint8),
+             lambda d: T.land2c[:, blk(d)].bitcast(dt.uint8), sem.p2)
+        if i == 0:
+            g.wait_ge(sem.pk2s, 1)
+        send(grp, lambda d: T.slot2s[:, SW * d:SW * d + CAP], lambda d: T.land2s[:, blk(d)], sem.p2)
+
+    Y.wait_ge(sem.srz, 2)
+    Y.wait_ge(sem.stst, 16)
+    Y.wait_ge(sem.sls, nst)
+    for q in range(8):
+        Y.dma_start(T.srow[16 * q:16 * q + 1, :], T.sland[:]).then_inc(sem.srl, 16)
+    V.wait_ge(sem.srl, 128)
+    V.wait_ge(sem.srz, 2)
+    cp(T.sg2[:], T.srow[:].indirect(T.off3[:]))
+    vw()
+    v(V.transpose(T.tr3[:], T.sg2[:]))
+    vw()
+    ts(T.pt[:, 0:32:2], T.tr3[:, 0:512:32], -float(T0 * me), None, A.add)
+    ts(T.pt[:, 1:32:2], T.tr3[:, 16:512:32], -float(T0 * me), None, A.add)
+    vw()
+    ts(T.pg[:], T.pt[:], float(T0), 16384.0, A.is_ge, A.mult)
+    vw()
+    tt(T.pu[:], T.pt[:], T.pg[:], A.add)
+    vw()
+    tt(T.pl[:], T.pu[:], T.dumpc[:], A.min)
+    vw()
+    ts(T.ph[:], T.pl[:], 0x7FF0, None, A.bitwise_and)
+    vw()
+    tt(T.pw[:], T.pl[:], T.ph[:], A.add)
+    vw()
+    ts(T.off4[:], T.pw[:], T.par16[:], None, A.add)
+    vw()
+    V.wait_ge(sem.srz, 2)
+    cp(T.win2[:].indirect(T.off4[:]), T.val[:])
+    vw()
+    v(V.transpose(T.tr2[:], T.win2[:, 0:768]))
+    vw()
+    tt(T.G2[:], T.tr2[:, 0:768:32], T.tr2[:, 16:768:32], A.add)
+    vw()
+    ts(T.off5[:], T.G2[:], 200.0, None, A.add, None, "off5s")
+
+    for s_, n_ in (("p2", incoming(2)), ("own2c", 1), ("own2s", 1), ("qws", 1)):
+        TE.wait_ge(sem[s_], n_)
+    for b in range(2):
+        TE.matmul_mx(T.ps[:, 512 * b:512 * b + H2], T.qw[:], T.sw[:], T.land2c[:, H2 * b:H2 * b + H2],
+                     T.land2s[:, H2 * b:H2 * b + H2], True, True).then_inc(sem["mm%d" % b], 1)
+    V.wait_ge(sem.mm0, 1)
+    cp(T.ysb[:, 0:H2], T.ps[:, 0:H2], "cpv")
+    S.wait_ge(sem.mm1, 1)
+    S.activation(T.ysb[:, H2:L2], T.ps[:, 512:512 + H2], AF.Copy).then_inc(sem.cps, 1)
+    for q in (V, S):
+        q.wait_ge(sem.off5s, 1)
+        q.wait_ge(sem.cpv, 1)
+        q.wait_ge(sem.cps, 1)
+    cp(T.yo[:, 0:192], T.ysb[:].indirect(T.off5[:, 0:12]), "yv")
+    S.activation(T.yo[:, 192:384], T.ysb[:].indirect(T.off5[:, 12:24]), AF.Copy).then_inc(sem.ys, 1)
+    Y.wait_ge(sem.yv, 1)
+    Y.dma_start(T.y[:, 0:192], T.yo[:, 0:192]).then_inc(sem.yst, 16)
+    S.wait_ge(sem.ys, 1)
+    S.dma_start(T.y[:, 192:384], T.yo[:, 192:384]).then_inc(sem.yst, 16)
+    Y.wait_ge(sem.yst, 32)
+    g.wait_ge(sem.loc, ln[0])

@@ -2,47 +2,48 @@ from concourse.bass import DstId, RemoteDMATransfer
 from concourse.mybir import dt, AluOpType as A, ActivationFunctionType as AF
 
 T0, N, Q1, CAP, SW = 384, 8, 48, 56, 64
+R1 = Q1 + 1
 OWN = 64
 L2 = OWN + 7 * CAP
-H2 = L2 // 2
-PAD = 8192.0
+L1 = L2 - 2 * CAP
+PK = 8192
+BIG = 65536.0
 X4, U8, U16, F32, BF, I32 = "float8_e4m3fn_x4", "uint8", "uint16", "float32", "bfloat16", "int32"
 
 
 def sb(n, t):
-    return ("sbuf", [128] + (list(n) if isinstance(n, (list, tuple)) else [n]), t)
+    return ("sbuf", [128, n], t)
 
 
 SCRATCH = {
     "xt": sb(1536, BF), "wt": sb(512, BF), "qx": sb(T0, X4), "sx": sb(T0, U8), "qw": sb(128, X4), "sw": sb(128, U8),
-    "slot1c": sb(T0, X4), "slot1s": sb(T0, U8), "land1c": sb(T0, X4), "land1s": sb(T0, U8),
+    "slot1c": sb(400, X4), "slot1s": sb(400, U8), "land1c": sb(512, X4), "land1s": sb(512, U8),
     "slot2c": sb(512, X4), "slot2s": sb(512, U8), "land2c": sb(L2, X4), "land2s": sb(L2, U8),
-    "tab": sb(24, I32), "key": sb(24, I32), "M": sb(192, F32), "M2": sb(192, F32), "Mm": sb(8, F32), "W": sb(192, F32),
-    "z192": sb(192, F32), "rst": sb(192, F32), "rst32": sb(32, F32), "tabf": sb(32, F32), "trr": sb(32, F32),
-    "torow": sb(512, F32), "tin": sb(32, F32), "tt0": sb(32, F32), "Qs": sb(32, F32), "tb": sb(96, F32),
-    "tb2": sb(96, F32), "F": sb(8, F32), "S": sb(192, F32), "Z": sb(192, F32), "Z1": sb(96, F32), "Z2": sb(48, F32),
-    "P": sb(24, I32), "u1": sb(24, I32), "w1": sb(24, F32), "off1": sb(24, U16), "cval": sb(T0, BF),
-    "win1": sb(768, BF), "tr1": sb(768, BF), "G": sb(24, F32), "g1": sb(24, U16), "ofp": sb(32, U16),
-    "sg": sb(512, F32), "srow": sb(4096, F32),
-    "pidx": sb(4, I32), "pi15": sb(4, I32), "pi16": sb(4, I32), "par128": sb(1, F32), "par16": sb(1, F32),
-    "par1": sb(1, F32), "k16": sb(4, F32), "fl4": sb(4, F32), "kp": sb(4, F32), "kt": sb(4, F32), "kpo": sb(4, F32),
-    "cstA": sb(64, F32), "c4096": sb(8, F32), "clampc": sb(32, F32), "dumpc": sb(32, F32),
-    "st": sb(64, U16), "stf": sb(64, F32), "nn": sb(64, F32), "ci": sb(64, I32), "c8p": sb(128, I32),
-    "e1p": sb(128, F32), "e2p": sb(128, F32), "B": sb(64, F32), "x1": sb(64, F32), "x2": sb(64, F32), "ai": sb(64, I32),
-    "ti": sb(64, I32), "J": sb(64, F32), "cm": sb((4, 64), F32), "pr": sb((4, 64), F32), "t1": sb((4, 32), F32),
-    "t2": sb((4, 16), F32), "t3": sb((4, 8), F32), "off2": sb(32, U16),
-    "y1": sb(8, F32), "y2": sb(8, F32), "a2": sb((8, 8), I32), "ti2": sb((8, 8), I32), "J2": sb((8, 8), F32),
-    "Bx": sb((8, 8), F32), "cm2": sb((32, 8), F32), "pr2": sb((32, 8), F32), "v1": sb((32, 4), F32),
-    "v2": sb((32, 2), F32), "v3": sb((4, 8), F32), "o3a": sb(32, F32), "o3b": sb(32, F32), "off3": sb(32, U16),
-    "sg2": sb(512, F32), "tr3": sb(512, F32), "pt": sb(32, F32), "pg": sb(32, F32), "pu": sb(32, F32), "pl": sb(32, I32),
-    "ph": sb(32, I32), "pw": sb(32, F32), "off4": sb(32, U16), "locA": sb(512, F32), "locF": sb(512, F32),
-    "locO": sb(512, F32), "val": sb(512, BF), "win2": sb(2048, BF), "tr2": sb(768, BF), "G2": sb(24, F32),
+    "tab": sb(24, I32), "key": sb(24, I32), "thi": sb(24, I32), "M": sb(192, F32), "M2": sb(192, F32), "Mm": sb(8, F32),
+    "W": sb(192, F32), "z192": sb(192, F32), "rst": sb(192, F32), "rst32": sb(32, F32), "rst8": sb(64, F32),
+    "cc0": sb(24, F32), "cc": sb(24, F32), "tabx": sb(24, F32), "tabf": sb(32, F32), "trr": sb(32, F32),
+    "torow": sb(512, F32), "padr": sb(128, F32), "tin": sb(32, F32), "tt0": sb(32, F32),
+    "Qs": sb(32, F32), "tb": sb(96, F32), "tb2": sb(96, F32), "F": sb(8, F32), "S": sb(192, F32), "Z": sb(192, F32),
+    "Z1": sb(96, F32), "Z2": sb(48, F32), "P": sb(24, I32), "u1": sb(24, I32), "w1": sb(24, F32), "off1": sb(24, U16),
+    "win1": sb(768, F32), "tr1": sb(768, F32), "G": sb(24, I32), "gcol": sb(24, I32), "g1": sb(26, U16),
+    "ownl": sb(4, U16), "srow": sb(4096, F32), "zz": sb(768, BF),
+    "pidx": sb(4, I32), "pi15": sb(4, I32), "pi16": sb(4, I32), "par15": sb(1, F32), "par128": sb(1, F32),
+    "par16": sb(1, F32), "par1": sb(1, F32), "k16": sb(4, F32), "fl4": sb(4, F32), "kp": sb(4, F32), "kt": sb(4, F32),
+    "kpo": sb(4, F32), "kpo8": sb(4, F32), "nk": sb(4, F32), "nko8": sb(4, F32), "cA": sb(64, F32), "cA2": sb(64, F32),
+    "dumpc": sb(32, F32), "st": sb(64, U16), "stf": sb(72, F32), "nn": sb(64, I32), "ai": sb(64, I32), "ci": sb(64, I32),
+    "ti": sb(64, I32), "c8p": sb(66, F32), "nB": sb(64, F32), "ge": sb(256, F32), "tq": sb(64, F32), "sc": sb(256, F32),
+    "off2": sb(32, U16), "nBx": sb(64, F32), "stx": sb(64, F32), "ai2": sb(64, I32), "ti2": sb(64, I32),
+    "tq2": sb(64, F32), "ge2": sb(256, F32), "sc2": sb(256, F32), "off3": sb(32, U16),
+    "sg2": sb(512, F32), "tr3": sb(512, F32), "pd": sb(16, F32), "pe": sb(16, F32), "pt": sb(32, I32), "pq": sb(32, I32),
+    "pg": sb(32, F32), "pu": sb(32, F32), "pl": sb(32, F32), "off4": sb(32, U16),
+    "val": sb(512, BF), "win2": sb(6800, BF), "tr2": sb(768, BF), "G2": sb(24, F32),
     "off5": sb(24, U16), "ysb": sb(L2, F32), "yo": sb(T0, F32),
     "sland": ("dram", [8, 128, 4], F32), "ps": ("psum", [128, 1024], F32),
 }
-SEMAPHORES = ["vq", "sq", "gc1", "gc2", "lt", "lx", "lw", "ms", "m2", "trs", "torw", "sto", "qxs", "g1s", "pk1c", "pk1s",
-              "ofps", "own1s", "sgs", "stst", "srz", "wz", "off2s", "pk2c", "pk2s", "own2c", "own2s", "srl", "mm0", "mm1",
-              "cpv", "cps", "off5s", "yv", "ys", "yst", "qws", "sst", "sls", "p1", "p2", "loc"]
+SEMAPHORES = ["vq", "gc1", "gc2", "lt", "lx", "lw", "keyq", "ms", "m2", "trs", "torw", "sto", "qxs", "g1s", "pk1c", "pk1s",
+              "scq", "owns", "own1c", "own1s", "stst", "srz", "wz", "off2s", "pk2c", "pk2s", "own2c", "own2s", "srl",
+              "mm0", "mm1", "cpv", "cps", "off5s", "yv", "ys", "yst", "qws", "sst", "sls", "p1", "p2a", "p2b", "loc",
+              "zzs", "bq", "stq", "dupq", "valq", "w2s"]
 
 
 def plan(topo, ranks, r):
@@ -92,6 +93,9 @@ def rank_program(g, core, T, topo):
     def cp(out, in_, name=None):
         v(V.tensor_copy(out, in_), name)
 
+    def scan(out, a, b, o0, o1, name=None):
+        v(V.tensor_tensor_scan(out, a, b, 0.0, o0, o1), name)
+
     def dst(d):
         a = topo.addr(ranks[d])
         return DstId(rid=a[0], pnc=a[1])
@@ -102,75 +106,87 @@ def rank_program(g, core, T, topo):
         g.remote_dma_fused(ts_, local_sem=sem.loc)
         ln[0] += sum(bits(m) for _, m in group)
 
-    def incoming(calls):
-        return calls * sum(bits(m) for r in range(N) if r != me for grp in plan(topo, ranks, r) for d, m in grp if d == me)
+    def tell(piece, rsem):
+        g.remote_dma_fused([RemoteDMATransfer(dst_ids=[dst(d) for d in everyone], dma_engine_mask=all_mask, remote_sem=rsem,
+                                              srcs=[piece], dsts=[piece for d in everyone])], local_sem=sem.loc)
+        ln[0] += bits(all_mask)
+
+    plans = [plan(topo, ranks, r) for r in range(N)]
+
+    def incoming(i):
+        return 2 * sum(bits(m) for r in range(N) if r != me for d, m in plans[r][i] if d == me)
+
+    def base(s, d):
+        order = [q for i in range(2) for k in range(1, N) for q in [(d + k) % N] if d in [x for x, _ in plans[q][i]]]
+        return 0 if s == d else OWN + CAP * order.index(s)
 
     far_d = [d for d in range(N) if topo.chip(ranks[d]) != topo.chip(core)][0]
     all_mask = topo.mask(core, ranks[far_d])
     everyone = [(me + i) % N for i in range(1, N)]
+    nst = bits(all_mask) * (N - 1)
+    groups = plans[me]
 
     for q in range(8):
         (Y if q % 2 == 0 else S).dma_start(T.tab[16 * q:16 * q + 16, :], T.to[:]).then_inc(sem.lt, 16)
     S.dma_start(T.xt[:], T.x[:]).then_inc(sem.lx, 16)
     Y.dma_start(T.wt[:], T.w[:]).then_inc(sem.lw, 16)
 
-    def iota(out, pat, base, cm, s):
-        (g.iota(out, pat, base, cm) if s[1] else
-         g.iota(out, pat, base, cm, allow_small_or_imprecise_dtypes=True)).then_inc(sem[s[0]], 1)
-    iota(T.pidx[:], [[0, 4]], 0, 1, ("gc1", True))
-    iota(T.cval[:], [[1, T0]], -192, 0, ("gc1", False))
-    c2 = ("gc2", False)
-    iota(T.k16[:], [[16, 4]], 0, 0, c2)
-    iota(T.fl4[:], [[0, 2], [-32, 2]], 16, 0, c2)
-    iota(T.cstA[:], [[T0, 8], [0, 8]], 7 - me, 0, c2)
-    iota(T.c4096[:], [[4096, 8]], 0, 0, c2)
-    iota(T.clampc[:], [[64, 8], [0, 4]], 7 * 512 + 63, 0, c2)
-    iota(T.dumpc[:], [[16, 32]], T0, 1, c2)
-    iota(T.locF[:], [[0, 16], [-32, 2], [0, 16]], 16, 0, c2)
-    ng2 = 7
-    for lo, hi in ((0, me), (me, me + 1), (me + 1, N)):
-        if lo < hi:
-            b = 0 if lo == me else OWN + CAP * ((lo - me - 1) % N)
-            iota(T.locA[:, SW * lo:SW * hi], [[CAP, hi - lo], [1, SW]], b - 200, 0, c2)
-            ng2 += 1
+    def iota(out, pat, b, cm, s):
+        g.iota(out, pat, b, cm, allow_small_or_imprecise_dtypes=True).then_inc(sem[s], 1)
+    g.iota(T.pidx[:], [[0, 4]], 0, 1).then_inc(sem.gc1, 1)
+    iota(T.cc0[:], [[16, 24]], 0, 0, "gc1")
+    iota(T.k16[:], [[16, 4]], 0, 0, "gc2")
+    iota(T.fl4[:], [[0, 2], [-32, 2]], 16, 0, "gc2")
+    iota(T.cA[:], [[0, 8], [512, 8]], 7 - me, 0, "gc2")
+    iota(T.cA2[:], [[-1, 8], [512, 8]], 7, 0, "gc2")
+    iota(T.dumpc[:], [[16, 32]], 2 * N * T0, 1, "gc2")
 
-    v(V.memset(T.tabf[:], PAD))
+    v(V.memset(T.zz[:], 0.0), "zzs")
+    v(V.memset(T.padr[:], float(PK - 1)), "wz")
+    v(V.memset(T.torow[:], 0.0), "wz")
+    v(V.memset(T.tabf[:], 0.0))
     v(V.memset(T.tin[:], 0.0))
     v(V.memset(T.z192[:], 0.0))
     v(V.memset(T.rst[:], 1.0))
     v(V.memset(T.rst32[:], 1.0))
-    v(V.memset(T.torow[:], 0.0), "wz")
-    v(V.memset(T.win1[:], 0.0))
-    v(V.memset(T.c8p[:, 0:64], 0))
-    v(V.memset(T.e1p[:, 0:64], 0.0))
-    v(V.memset(T.e2p[:, 0:64], 0.0))
-    v(V.memset(T.ofp[:], T0))
-    vw()
-    v(V.memset(T.rst[:, 0:192:24], 0.0))
-    v(V.memset(T.rst32[:, 0:32:16], 0.0))
+    v(V.memset(T.g1[:], 0))
+    v(V.memset(T.ownl[:], 0))
     V.wait_ge(sem.gc1, 2)
     ts(T.pi15[:], T.pidx[:], 15, None, A.bitwise_and)
     ts(T.pi16[:], T.pidx[:], 16, None, A.bitwise_and)
     vw()
+    v(V.memset(T.rst[:, 0:192:24], 0.0))
+    v(V.memset(T.rst32[:, 0:32:16], 0.0))
+    ts(T.par15[:], T.pi15[:, 0:1], 1.0, None, A.mult)
     ts(T.par128[:], T.pi16[:, 0:1], 8.0, None, A.mult)
-    ts(T.par16[:], T.pi16[:, 0:1], 1.0, None, A.mult)
-    ts(T.par1[:], T.pi16[:, 0:1], 0.0625, None, A.mult)
+    vw()
+    ts(T.cc[:], T.cc0[:], T.par15[:], float(PK), A.add, A.mult)
+    v(V.memset(T.win1[:], 0.0))
+    vw()
+    S.wait_ge(sem.zzs, 1)
+    for h in range(3):
+        S.activation(T.srow[:, 768 * h:768 * h + 768], T.zz[:], AF.Copy).then_inc(sem.srz, 1)
 
     V.wait_ge(sem.lt, 128)
-    ts(T.key[:], T.tab[:], 1.0 / T0, 0.5 / T0 - 0.5, A.mult, A.add)
-    vw()
+    ts(T.key[:], T.tab[:], 1.0 / T0, 0.5 / T0 - 0.5, A.mult, A.add, "keyq")
+    ts(T.thi[:], T.tab[:], 0xFF0, None, A.bitwise_and)
+    tt(T.tabx[:], T.tab[:], T.cc[:], A.add)
+    V.wait_ge(sem.keyq, 1)
     for d in range(N):
+        if d == 3:
+            vw()
+            tt(T.tabf[:, 0:24], T.tabx[:], T.thi[:], A.add)
         ts(T.M[:, 24 * d:24 * d + 24], T.key[:], float(d), None, A.is_equal, None, "ms")
-    cp(T.tabf[:, 0:24], T.tab[:])
+    vw()
+    v(V.transpose(T.trr[:], T.tabf[:]), "trs")
     V.wait_ge(sem.ms, N)
-    v(V.tensor_tensor_scan(T.W[:], T.M[:], T.z192[:], 0.0, A.add, A.add))
+    scan(T.W[:], T.M[:], T.z192[:], A.add, A.add)
     vw()
     cp(T.tin[:, 1:9], T.W[:, 23:192:24])
-    v(V.transpose(T.trr[:], T.tabf[:]), "trs")
     vw()
     v(V.transpose(T.tt0[:], T.tin[:]))
     vw()
-    v(V.tensor_tensor_scan(T.Qs[:], T.rst32[:], T.tt0[:], 0.0, A.mult, A.add))
+    scan(T.Qs[:], T.rst32[:], T.tt0[:], A.mult, A.add)
     vw()
     tt(T.tb[:, 32:64], T.Qs[:], T.tt0[:], A.subtract)
     ts(T.tb[:, 64:96], T.Qs[:], 0.0, T.Qs[:, 15:16], A.mult, A.add)
@@ -179,8 +195,8 @@ def rank_program(g, core, T, topo):
     vw()
     v(V.transpose(T.tb2[:], T.tb[:]))
     vw()
-    tt(T.F[:], T.tb2[:, 0:8], T.tb2[:, 33:41], A.add)
     cp(T.st[:, 8 * me:8 * me + 8], T.tb2[:, 64:72], "sto")
+    tt(T.F[:], T.tb2[:, 0:8], T.tb2[:, 33:41], A.add)
     S.wait_ge(sem.ms, N)
     S.activation(T.M2[:], T.M[:], AF.Copy).then_inc(sem.m2, 1)
     S.activation(T.Mm[:], T.M[:, 0:192:24], AF.Identity, -1.0).then_inc(sem.m2, 1)
@@ -188,7 +204,7 @@ def rank_program(g, core, T, topo):
     vw()
     tt(T.M2[:, 0:192:24], T.Mm[:], T.F[:], A.add)
     vw()
-    v(V.tensor_tensor_scan(T.S[:], T.rst[:], T.M2[:], 0.0, A.mult, A.add))
+    scan(T.S[:], T.rst[:], T.M2[:], A.mult, A.add)
     vw()
     tt(T.Z[:], T.S[:], T.M[:], A.mult)
     vw()
@@ -203,210 +219,200 @@ def rank_program(g, core, T, topo):
     tt(T.w1[:], T.P[:], T.u1[:], A.add)
     vw()
     ts(T.off1[:], T.w1[:], T.par128[:], None, A.add)
+    Y.wait_ge(sem.wz, 2)
+    Y.dma_start(T.sland[me, 96:128, :], T.padr[0:1, :]).then_inc(sem.stst, 16)
+    Y.wait_ge(sem.trs, 1)
+    for q in range(8):
+        Y.dma_start(T.torow[16 * q:16 * q + 1, :], T.trr[32 * (q // 2):32 * (q // 2) + 32, 0:16]).then_inc(sem.torw, 16)
+    V.wait_ge(sem.torw, 128)
+    V.wait_ge(sem.wz, 2)
     vw()
-    cp(T.win1[:, 0:768].indirect(T.off1[:, 0:24]), T.cval[:])
+    cp(T.win1[:, 0:768].indirect(T.off1[:, 0:24]), T.torow[:, 0:T0], "scq")
     V.wait_ge(sem.lx, 16)
     v(V.quantize_mx(T.qx[:], T.sx[:], T.xt[:]), "qxs")
-    vw()
+    V.wait_ge(sem.scq, 1)
     for m in range(N):
         v(V.transpose(T.tr1[:, 96 * m:96 * m + 96], T.win1[:, m:768:8]))
     vw()
     tt(T.G[:], T.tr1[:, 0:768:32], T.tr1[:, 16:768:32], A.add)
     vw()
-    ts(T.g1[:], T.G[:], 192.0, None, A.add, None, "g1s")
+    ts(T.gcol[:], T.G[:], 13, None, A.arith_shift_right)
+    vw()
+    cp(T.g1[:, 0:24], T.gcol[:], "g1s")
+    cp(T.ownl[:, 0:3], T.gcol[:, 3 * me:3 * me + 3], "owns")
     V.wait_ge(sem.g1s, 1)
     V.wait_ge(sem.qxs, 1)
-    cp(T.slot1c[:].bitcast(dt.uint32), T.qx[:].bitcast(dt.uint32).indirect(T.g1[:, 0:24]), "pk1c")
+    cp(T.slot1c[:].bitcast(dt.uint32), T.qx[:].bitcast(dt.uint32).indirect(T.g1[:, 0:25]), "pk1c")
     S.wait_ge(sem.g1s, 1)
     S.wait_ge(sem.qxs, 1)
-    S.activation(T.slot1s[:], T.sx[:].indirect(T.g1[:, 0:24]), AF.Copy).then_inc(sem.pk1s, 1)
+    S.activation(T.slot1s[:], T.sx[:].indirect(T.g1[:, 0:25]), AF.Copy).then_inc(sem.pk1s, 1)
+    V.wait_ge(sem.owns, 1)
+    own1 = slice(SW * me, SW * me + SW)
+    cp(T.land1c[:, own1].bitcast(dt.uint32), T.qx[:].bitcast(dt.uint32).indirect(T.ownl[:]), "own1c")
+    S.wait_ge(sem.owns, 1)
+    S.activation(T.land1s[:, own1], T.sx[:].indirect(T.ownl[:]), AF.Copy).then_inc(sem.own1s, 1)
+    Y.wait_ge(sem.scq, 1)
     for h in range(3):
-        ts(T.ofp[:, h:32:4], T.G[:, h:24:3], 192.0, None, A.add, None, "ofps")
-    V.wait_ge(sem.ofps, 3)
-    cp(T.land1c[:, Q1 * me:Q1 * me + Q1].bitcast(dt.uint32),
-       T.qx[:].bitcast(dt.uint32).indirect(T.ofp[:, 4 * me:4 * me + 3]))
-    S.wait_ge(sem.ofps, 3)
-    S.activation(T.land1s[:, Q1 * me:Q1 * me + Q1], T.sx[:].indirect(T.ofp[:, 4 * me:4 * me + 3]), AF.Copy).then_inc(sem.own1s, 1)
+        Y.dma_start(T.sland[me, 32 * h:32 * h + 32, :], T.win1[0:1, 256 * h:256 * h + 128]).then_inc(sem.stst, 16)
 
     g.wait_ge(sem.sto, 1)
-    g.remote_dma_fused([RemoteDMATransfer(dst_ids=[dst(d) for d in everyone], dma_engine_mask=all_mask, remote_sem=sem.sst,
-                                          srcs=[T.st[:, 8 * me:8 * me + 8]], dsts=[T.st[:, 8 * me:8 * me + 8] for d in everyone])],
-                       local_sem=sem.loc)
-    ln[0] += bits(all_mask)
-    groups = plan(topo, ranks, me)
+    tell(T.st[:, 8 * me:8 * me + 8], sem.sst)
+    land1 = slice(SW * me, SW * me + R1)
+
+    def codes1(grp):
+        send(grp, lambda d: T.slot1c[:, Q1 * d:Q1 * d + R1].bitcast(dt.uint8), lambda d: T.land1c[:, land1].bitcast(dt.uint8), sem.p1)
+
+    def scales1(grp):
+        send(grp, lambda d: T.slot1s[:, Q1 * d:Q1 * d + R1], lambda d: T.land1s[:, land1], sem.p1)
     g.wait_ge(sem.pk1c, 1)
-    for i, grp in enumerate(groups):
-        send(grp, lambda d: T.slot1c[:, Q1 * d:Q1 * d + Q1].bitcast(dt.uint8),
-             lambda d: T.land1c[:, Q1 * me:Q1 * me + Q1].bitcast(dt.uint8), sem.p1)
-        if i == 0:
-            g.wait_ge(sem.pk1s, 1)
-        send(grp, lambda d: T.slot1s[:, Q1 * d:Q1 * d + Q1], lambda d: T.land1s[:, Q1 * me:Q1 * me + Q1], sem.p1)
+    codes1(groups[0])
+    codes1(groups[1])
+    g.wait_ge(sem.stst, 64)
+    tell(T.sland[me], sem.sls)
+    g.wait_ge(sem.pk1s, 1)
+    scales1(groups[0])
+    scales1(groups[1])
+    for m in range(N):
+        iota(T.val[:, SW * m:SW * m + SW], [[1, SW]], base(m, me) - 200, 0, "valq")
 
-    Y.wait_ge(sem.trs, 1)
-    Y.wait_ge(sem.wz, 1)
-    Y.dma_start(T.torow[0:1, :], T.trr[0:32, 0:16]).then_inc(sem.torw, 16)
-    S.wait_ge(sem.torw, 16)
-    S.wait_ge(sem.wz, 1)
-    S.activation(T.sg[:], T.torow[:].indirect(T.ofp[:]), AF.Copy).then_inc(sem.sgs, 1)
-    Y.wait_ge(sem.sgs, 1)
-    Y.dma_start(T.sland[me], T.sg[0:1, :]).then_inc(sem.stst, 16)
-    g.wait_ge(sem.stst, 16)
-    g.remote_dma_fused([RemoteDMATransfer(dst_ids=[dst(d) for d in everyone], dma_engine_mask=all_mask, remote_sem=sem.sls,
-                                          srcs=[T.sland[me]], dsts=[T.sland[me] for d in everyone])], local_sem=sem.loc)
-    ln[0] += bits(all_mask)
-
-    v(V.memset(T.win2[:], 0.0), "off2s")
-    V.wait_ge(sem.gc2, ng2)
-    ts(T.locO[:], T.locF[:], T.par1[:], None, A.mult)
+    w2 = slice(2 * T0 * me, 2 * T0 * me + 2 * T0)
+    v(V.memset(T.stf[:, 64:72], float(T0)))
+    v(V.memset(T.c8p[:], 0.0))
+    v(V.memset(T.rst8[:], 1.0))
+    ts(T.par1[:], T.pi16[:, 0:1], 0.0625, None, A.mult)
+    ts(T.par16[:], T.pi16[:, 0:1], 1.0, None, A.mult)
+    V.wait_ge(sem.gc2, 5)
     tt(T.kp[:], T.pi15[:], T.k16[:], A.add)
+    vw()
+    v(V.memset(T.rst8[:, 0:64:8], 0.0))
     ts(T.kt[:], T.fl4[:], T.par1[:], None, A.mult)
+    ts(T.nk[:], T.kp[:], -1.0, None, A.mult)
+    v(V.memset(T.win2[:, w2], 0.0), "w2s")
     vw()
     tt(T.kpo[:], T.kp[:], T.kt[:], A.add)
-    tt(T.val[:], T.locA[:], T.locO[:], A.add)
-    S.wait_ge(sem.off2s, 1)
-    for h in range(2):
-        S.activation(T.srow[:, 2048 * h:2048 * h + 2048], T.win2[:], AF.Copy).then_inc(sem.srz, 1)
     V.wait_ge(sem.lw, 16)
     v(V.quantize_mx(T.qw[:], T.sw[:], T.wt[:]), "qws")
+    vw()
+    ts(T.kpo8[:], T.kpo[:], 8.0, None, A.mult)
+    ts(T.nko8[:], T.kpo[:], -8.0, None, A.mult)
 
-    nst = bits(all_mask) * (N - 1)
     V.wait_ge(sem.sst, nst)
     V.wait_ge(sem.sto, 1)
-    cp(T.stf[:], T.st[:])
+    for d in range(N):
+        cp(T.stf[:, 8 * d:8 * d + 8], T.st[:, d:64:8], "stq")
+    V.wait_ge(sem.stq, N)
     vw()
-    tt(T.nn[:, 0:63], T.stf[:, 1:64], T.stf[:, 0:63], A.subtract)
+    tt(T.nn[:], T.stf[:, 0:64], T.stf[:, 8:72], A.subtract)
+    tt(T.ai[:], T.stf[:, 0:64], T.cA[:], A.add)
     vw()
-    ts(T.nn[:, 7:64:8], T.stf[:, 7:64:8], -1.0, float(T0), A.mult, A.add)
-    vw()
-    ts(T.ci[:], T.nn[:], 7.0, None, A.add)
-    vw()
-    ts(T.c8p[:, 64:128], T.ci[:], 3, None, A.arith_shift_right)
-    vw()
-    tt(T.e1p[:, 64:128], T.c8p[:, 56:120], T.c8p[:, 48:112], A.add)
-    vw()
-    tt(T.e2p[:, 64:128], T.e1p[:, 64:128], T.e1p[:, 48:112], A.add)
-    vw()
-    tt(T.B[:], T.e2p[:, 64:128], T.e2p[:, 32:96], A.add)
-    tt(T.x2[:], T.cstA[:], T.stf[:], A.add)
-    tt(T.y2[:], T.c4096[:], T.stf[:, me:64:8], A.add)
-    vw()
-    ts(T.x1[:], T.B[:], -8.0, None, A.mult)
-    vw()
-    tt(T.ai[:], T.x1[:], T.x2[:], A.add)
-    for kk in range(4):
-        ts(T.cm[:, kk, :], T.B[:], T.kp[:, kk:kk + 1], None, A.is_le)
-    vw()
+    ts(T.ci[:], T.nn[:], 3, None, A.arith_shift_right)
     ts(T.ti[:], T.ai[:], 3, None, A.arith_shift_right)
-    tt(T.y1[:], T.x1[:, me:64:8], T.y2[:], A.add)
     vw()
-    tt(T.J[:, 8:64], T.ti[:, 8:64], T.ti[:, 0:56], A.subtract)
-    cp(T.J[:, 0:8], T.ti[:, 0:8])
+    cp(T.c8p[:, 1:65], T.ci[:])
+    vw()
+    scan(T.nB[:], T.c8p[:, 0:64], T.rst8[:], A.add, A.mult, "bq")
+    V.wait_ge(sem.bq, 1)
+    tt(T.tq[:], T.ti[:], T.nB[:], A.add)
+    for kk in range(4):
+        ts(T.ge[:, 64 * kk:64 * kk + 64], T.nB[:], T.nk[:, kk:kk + 1], BIG, A.is_ge, A.mult)
     vw()
     for kk in range(4):
-        tt(T.pr[:, kk, :], T.cm[:, kk, :], T.J[:], A.mult)
-    vw()
-    tt(T.t1[:], T.pr[:, :, 0:32], T.pr[:, :, 32:64], A.add)
-    vw()
-    tt(T.t2[:], T.t1[:, :, 0:16], T.t1[:, :, 16:32], A.add)
-    vw()
-    tt(T.t3[:], T.t2[:, :, 0:8], T.t2[:, :, 8:16], A.add)
+        scan(T.sc[:, 64 * kk:64 * kk + 64], T.ge[:, 64 * kk:64 * kk + 64], T.tq[:], A.max, A.min)
     vw()
     for kk in range(4):
-        ts(T.off2[:, kk:32:4], T.t3[:, kk, :], T.kp[:, kk:kk + 1], float(T0 - 1), A.add, A.min, "off2s")
+        ts(T.off2[:, kk:32:4], T.sc[:, 64 * kk + 7:64 * kk + 64:8], T.kp[:, kk:kk + 1], float(7 * SW + Q1), A.add, A.min, "off2s")
+    S.wait_ge(sem.stq, N)
     for m in range(N):
-        ts(T.a2[:, m, :], T.y1[:], float(7 - m + 512 * m), None, A.add)
-        cp(T.Bx[:, m, :], T.B[:, me:64:8])
-    vw()
-    ts(T.ti2[:], T.a2[:], 3, None, A.arith_shift_right)
+        S.activation(T.stx[:, 8 * m:8 * m + 8], T.stf[:, 8 * me:8 * me + 8], AF.Copy).then_inc(sem.dupq, 1)
+    S.wait_ge(sem.bq, 1)
+    for m in range(N):
+        S.activation(T.nBx[:, 8 * m:8 * m + 8], T.nB[:, 8 * me:8 * me + 8], AF.Identity, float(m), 8.0).then_inc(sem.dupq, 1)
+    for lo, hi in ((2304, 3072), (3072, 3840), (3840, 4096)):
+        S.activation(T.srow[:, lo:hi], T.zz[:, 0:hi - lo], AF.Copy).then_inc(sem.srz, 1)
+    V.wait_ge(sem.dupq, 2 * N)
+    tt(T.ai2[:], T.stx[:], T.cA2[:], A.add)
     for kk in range(4):
-        ts(T.cm2[:, 8 * kk:8 * kk + 8, :], T.Bx[:], T.kpo[:, kk:kk + 1], None, A.is_le)
+        ts(T.ge2[:, 64 * kk:64 * kk + 64], T.nBx[:], T.nko8[:, kk:kk + 1], BIG, A.is_ge, A.mult)
     vw()
-    tt(T.J2[:, :, 1:8], T.ti2[:, :, 1:8], T.ti2[:, :, 0:7], A.subtract)
-    cp(T.J2[:, :, 0:1], T.ti2[:, :, 0:1])
+    ts(T.ti2[:], T.ai2[:], 0xFFF8, None, A.bitwise_and)
     vw()
-    for kk in range(4):
-        tt(T.pr2[:, 8 * kk:8 * kk + 8, :], T.cm2[:, 8 * kk:8 * kk + 8, :], T.J2[:], A.mult)
-    vw()
-    tt(T.v1[:], T.pr2[:, :, 0:4], T.pr2[:, :, 4:8], A.add)
-    vw()
-    tt(T.v2[:], T.v1[:, :, 0:2], T.v1[:, :, 2:4], A.add)
+    tt(T.tq2[:], T.ti2[:], T.nBx[:], A.add)
     vw()
     for kk in range(4):
-        tt(T.v3[:, kk, :], T.v2[:, 8 * kk:8 * kk + 8, 0], T.v2[:, 8 * kk:8 * kk + 8, 1], A.add)
+        scan(T.sc2[:, 64 * kk:64 * kk + 64], T.ge2[:, 64 * kk:64 * kk + 64], T.tq2[:], A.max, A.min)
     vw()
     for kk in range(4):
-        ts(T.o3a[:, kk:32:4], T.v3[:, kk, :], T.kpo[:, kk:kk + 1], None, A.add)
-    vw()
-    tt(T.o3b[:], T.o3a[:], T.clampc[:], A.min)
-    vw()
-    cp(T.off3[:], T.o3b[:])
+        ts(T.off3[:, kk:32:4], T.sc2[:, 64 * kk + 7:64 * kk + 64:8], T.kpo8[:, kk:kk + 1], 4095.0, A.add, A.min)
 
-    V.wait_ge(sem.off2s, 5)
-    V.wait_ge(sem.p1, incoming(2))
-    vw()
+    V.wait_ge(sem.off2s, 4)
+    V.wait_ge(sem.own1c, 1)
+    V.wait_ge(sem.p1, incoming(0) + incoming(1))
     cp(T.slot2c[:].bitcast(dt.uint32), T.land1c[:].bitcast(dt.uint32).indirect(T.off2[:]), "pk2c")
     cp(T.land2c[:, 0:OWN].bitcast(dt.uint32), T.land1c[:].bitcast(dt.uint32).indirect(T.off2[:, 4 * me:4 * me + 4]), "own2c")
-    S.wait_ge(sem.off2s, 5)
-    S.wait_ge(sem.p1, incoming(2))
+    S.wait_ge(sem.off2s, 4)
+    S.wait_ge(sem.p1, incoming(0) + incoming(1))
     S.wait_ge(sem.own1s, 1)
     S.activation(T.slot2s[:], T.land1s[:].indirect(T.off2[:]), AF.Copy).then_inc(sem.pk2s, 1)
     S.activation(T.land2s[:, 0:OWN], T.land1s[:].indirect(T.off2[:, 4 * me:4 * me + 4]), AF.Copy).then_inc(sem.own2s, 1)
 
     def blk(d):
-        a = OWN + CAP * ((me - d - 1) % N)
-        return slice(a, a + CAP)
+        return slice(base(me, d), base(me, d) + CAP)
     g.wait_ge(sem.pk2c, 1)
     for i, grp in enumerate(groups):
+        rs = sem["p2" + "ab"[i]]
         send(grp, lambda d: T.slot2c[:, SW * d:SW * d + CAP].bitcast(dt.uint8),
-             lambda d: T.land2c[:, blk(d)].bitcast(dt.uint8), sem.p2)
+             lambda d: T.land2c[:, blk(d)].bitcast(dt.uint8), rs)
         if i == 0:
             g.wait_ge(sem.pk2s, 1)
-        send(grp, lambda d: T.slot2s[:, SW * d:SW * d + CAP], lambda d: T.land2s[:, blk(d)], sem.p2)
+        send(grp, lambda d: T.slot2s[:, SW * d:SW * d + CAP], lambda d: T.land2s[:, blk(d)], rs)
 
-    Y.wait_ge(sem.srz, 2)
-    Y.wait_ge(sem.stst, 16)
+    Y.wait_ge(sem.srz, 6)
+    Y.wait_ge(sem.stst, 64)
     Y.wait_ge(sem.sls, nst)
     for q in range(8):
         Y.dma_start(T.srow[16 * q:16 * q + 1, :], T.sland[:]).then_inc(sem.srl, 16)
     V.wait_ge(sem.srl, 128)
-    V.wait_ge(sem.srz, 2)
+    vw()
     cp(T.sg2[:], T.srow[:].indirect(T.off3[:]))
     vw()
     v(V.transpose(T.tr3[:], T.sg2[:]))
     vw()
-    ts(T.pt[:, 0:32:2], T.tr3[:, 0:512:32], -float(T0 * me), None, A.add)
-    ts(T.pt[:, 1:32:2], T.tr3[:, 16:512:32], -float(T0 * me), None, A.add)
+    tt(T.pd[:], T.tr3[:, 0:512:32], T.tr3[:, 16:512:32], A.subtract)
     vw()
-    ts(T.pg[:], T.pt[:], float(T0), 16384.0, A.is_ge, A.mult)
+    ts(T.pe[:], T.pd[:], T.par1[:], None, A.mult)
     vw()
-    tt(T.pu[:], T.pt[:], T.pg[:], A.add)
+    tt(T.pt[:, 0:32:2], T.tr3[:, 0:512:32], T.pe[:], A.subtract)
+    tt(T.pt[:, 1:32:2], T.tr3[:, 16:512:32], T.pe[:], A.add)
+    vw()
+    ts(T.pq[:], T.pt[:], PK - 1, None, A.bitwise_and)
+    vw()
+    ts(T.pg[:], T.pq[:], float(2 * T0 * me + 2 * T0), BIG, A.is_ge, A.mult)
+    vw()
+    tt(T.pu[:], T.pq[:], T.pg[:], A.add)
     vw()
     tt(T.pl[:], T.pu[:], T.dumpc[:], A.min)
     vw()
-    ts(T.ph[:], T.pl[:], 0x7FF0, None, A.bitwise_and)
+    ts(T.off4[:], T.pl[:], T.par16[:], None, A.add)
     vw()
-    tt(T.pw[:], T.pl[:], T.ph[:], A.add)
-    vw()
-    ts(T.off4[:], T.pw[:], T.par16[:], None, A.add)
-    vw()
-    V.wait_ge(sem.srz, 2)
+    V.wait_ge(sem.w2s, 1)
+    V.wait_ge(sem.valq, N)
     cp(T.win2[:].indirect(T.off4[:]), T.val[:])
     vw()
-    v(V.transpose(T.tr2[:], T.win2[:, 0:768]))
+    v(V.transpose(T.tr2[:], T.win2[:, w2]))
     vw()
     tt(T.G2[:], T.tr2[:, 0:768:32], T.tr2[:, 16:768:32], A.add)
     vw()
     ts(T.off5[:], T.G2[:], 200.0, None, A.add, None, "off5s")
 
-    for s_, n_ in (("p2", incoming(2)), ("own2c", 1), ("own2s", 1), ("qws", 1)):
+    for s_, n_ in (("p2a", incoming(0)), ("own2c", 1), ("own2s", 1), ("qws", 1)):
         TE.wait_ge(sem[s_], n_)
-    for b in range(2):
-        TE.matmul_mx(T.ps[:, 512 * b:512 * b + H2], T.qw[:], T.sw[:], T.land2c[:, H2 * b:H2 * b + H2],
-                     T.land2s[:, H2 * b:H2 * b + H2], True, True).then_inc(sem["mm%d" % b], 1)
-    V.wait_ge(sem.mm0, 1)
-    cp(T.ysb[:, 0:H2], T.ps[:, 0:H2], "cpv")
-    S.wait_ge(sem.mm1, 1)
-    S.activation(T.ysb[:, H2:L2], T.ps[:, 512:512 + H2], AF.Copy).then_inc(sem.cps, 1)
+    TE.matmul_mx(T.ps[:, 0:L1], T.qw[:], T.sw[:], T.land2c[:, 0:L1], T.land2s[:, 0:L1], True, True).then_inc(sem.mm0, 1)
+    TE.wait_ge(sem.p2b, incoming(1))
+    TE.matmul_mx(T.ps[:, 512:640], T.qw[:], T.sw[:], T.land2c[:, L2 - 128:L2], T.land2s[:, L2 - 128:L2], True, True).then_inc(sem.mm1, 1)
+    S.wait_ge(sem.mm0, 1)
+    S.activation(T.ysb[:, 0:L1], T.ps[:, 0:L1], AF.Copy).then_inc(sem.cps, 1)
+    V.wait_ge(sem.mm1, 1)
+    cp(T.ysb[:, L1:L2], T.ps[:, 640 - L2 + L1:640], "cpv")
     for q in (V, S):
         q.wait_ge(sem.off5s, 1)
         q.wait_ge(sem.cpv, 1)

@@ -6,7 +6,7 @@ R1 = Q1 + 1
 OWN = 64
 L2 = OWN + 7 * CAP
 L1 = L2 - 2 * CAP
-PK = 8192
+NOPL = 8191.0
 BIG = 65536.0
 X4, U8, U16, F32, BF, I32 = "float8_e4m3fn_x4", "uint8", "uint16", "float32", "bfloat16", "int32"
 
@@ -19,31 +19,39 @@ SCRATCH = {
     "xt": sb(1536, BF), "wt": sb(512, BF), "qx": sb(T0, X4), "sx": sb(T0, U8), "qw": sb(128, X4), "sw": sb(128, U8),
     "slot1c": sb(400, X4), "slot1s": sb(400, U8), "land1c": sb(512, X4), "land1s": sb(512, U8),
     "slot2c": sb(512, X4), "slot2s": sb(512, U8), "land2c": sb(L2, X4), "land2s": sb(L2, U8),
-    "tab": sb(24, I32), "key": sb(24, I32), "thi": sb(24, I32), "M": sb(192, F32), "M2": sb(192, F32), "Mm": sb(8, F32),
-    "W": sb(192, F32), "z192": sb(192, F32), "rst": sb(192, F32), "rst32": sb(32, F32), "rst8": sb(64, F32),
-    "cc0": sb(24, F32), "cc": sb(24, F32), "tabx": sb(24, F32), "tabf": sb(32, F32), "trr": sb(32, F32),
-    "torow": sb(512, F32), "padr": sb(128, F32), "tin": sb(32, F32), "tt0": sb(32, F32),
-    "Qs": sb(32, F32), "tb": sb(96, F32), "tb2": sb(96, F32), "F": sb(8, F32), "S": sb(192, F32), "Z": sb(192, F32),
-    "Z1": sb(96, F32), "Z2": sb(48, F32), "P": sb(24, I32), "u1": sb(24, I32), "w1": sb(24, F32), "off1": sb(24, U16),
-    "win1": sb(768, F32), "tr1": sb(768, F32), "G": sb(24, I32), "gcol": sb(24, I32), "g1": sb(26, U16),
-    "ownl": sb(4, U16), "srow": sb(4096, F32), "zz": sb(768, BF),
+    "relst": sb(8, U16), "rel1c": sb(R1, X4), "rel1s": sb(R1, U8), "rel2c": sb(CAP, X4), "rel2s": sb(CAP, U8),
+    "tab": sb(24, I32), "key": sb(24, I32), "tabk": sb(32, F32), "M": sb(192, F32),
+    "W": sb(816, F32), "z192": sb(192, F32), "rst32": sb(32, F32), "rst8": sb(64, F32),
+    "gd": sb(192, F32), "td": sb(192, F32), "pos": sb(192, F32), "trr": sb(32, F32),
+    "torc": sb(T0, F32), "padr": sb(128, F32), "tt0": sb(32, F32),
+    "Qs": sb(32, F32), "tb": sb(96, F32), "tb2": sb(96, F32), "F": sb(8, F32), "off1": sb(24, U16),
+    "win1": sb(512, F32), "tr1": sb(512, F32), "Ge": sb(32, F32), "Go": sb(32, F32), "G": sb(24, F32),
+    "g1": sb(26, U16), "ownl": sb(4, U16), "srow": sb(4096, F32), "zz": sb(768, BF),
     "pidx": sb(4, I32), "pi15": sb(4, I32), "pi16": sb(4, I32), "par15": sb(1, F32), "par128": sb(1, F32),
-    "par16": sb(1, F32), "par1": sb(1, F32), "k16": sb(4, F32), "fl4": sb(4, F32), "kp": sb(4, F32), "kt": sb(4, F32),
-    "kpo": sb(4, F32), "kpo8": sb(4, F32), "nk": sb(4, F32), "nko8": sb(4, F32), "cA": sb(64, F32), "cA2": sb(64, F32),
-    "dumpc": sb(32, F32), "st": sb(64, U16), "stf": sb(72, F32), "nn": sb(64, I32), "ai": sb(64, I32), "ci": sb(64, I32),
+    "par16": sb(1, F32), "par1": sb(1, F32), "epar": sb(1, F32), "k16": sb(4, F32), "fl4": sb(4, F32), "kp": sb(4, F32),
+    "kt": sb(4, F32), "kpo": sb(4, F32), "kpo8": sb(4, F32), "nk": sb(4, F32), "nko8": sb(4, F32), "cA": sb(64, F32),
+    "cA2": sb(64, F32), "st": sb(64, U16), "stf": sb(72, F32), "nn": sb(64, I32), "ai": sb(64, I32), "ci": sb(64, I32),
     "ti": sb(64, I32), "c8p": sb(66, F32), "nB": sb(64, F32), "ge": sb(256, F32), "tq": sb(64, F32), "sc": sb(256, F32),
     "off2": sb(32, U16), "nBx": sb(64, F32), "stx": sb(64, F32), "ai2": sb(64, I32), "ti2": sb(64, I32),
     "tq2": sb(64, F32), "ge2": sb(256, F32), "sc2": sb(256, F32), "off3": sb(32, U16),
-    "sg2": sb(512, F32), "tr3": sb(512, F32), "pd": sb(16, F32), "pe": sb(16, F32), "pt": sb(32, I32), "pq": sb(32, I32),
-    "pg": sb(32, F32), "pu": sb(32, F32), "pl": sb(32, F32), "off4": sb(32, U16),
-    "val": sb(512, BF), "win2": sb(6800, BF), "tr2": sb(768, BF), "G2": sb(24, F32),
-    "off5": sb(24, U16), "ysb": sb(L2, F32), "yo": sb(T0, F32),
+    "sg2": sb(512, F32), "tr3": sb(512, F32), "d0": sb(64, F32), "d1": sb(64, F32), "pl": sb(64, F32), "off4": sb(32, U16),
+    "val": sb(512, BF), "valo": sb(512, BF), "win2": sb(3712, BF), "tr2": sb(416, BF), "Ie": sb(26, F32),
+    "Io": sb(26, F32), "G2": sb(24, F32), "off5": sb(24, U16), "ysb": sb(L2, F32), "yo": sb(T0, F32),
     "sland": ("dram", [8, 128, 4], F32), "ps": ("psum", [128, 1024], F32),
 }
-SEMAPHORES = ["vq", "gc1", "gc2", "lt", "lx", "lw", "keyq", "ms", "m2", "trs", "torw", "sto", "qxs", "g1s", "pk1c", "pk1s",
-              "scq", "owns", "own1c", "own1s", "stst", "srz", "wz", "off2s", "pk2c", "pk2s", "own2c", "own2s", "srl",
-              "mm0", "mm1", "cpv", "cps", "off5s", "yv", "ys", "yst", "qws", "sst", "sls", "p1", "p2a", "p2b", "loc",
-              "zzs", "bq", "stq", "dupq", "valq", "w2s"]
+SEMAPHORES = ["vq", "gc1", "gct", "gc2", "lt", "lx", "lw", "keyq", "ms", "gds", "fs", "tds", "trs", "torw", "sto", "qxs",
+              "g1s", "pk1c", "pk1s", "scq", "owns", "own1c", "own1s", "stst", "srz", "wz", "off2s", "pk2c", "pk2s",
+              "own2c", "own2s", "srl", "mm0", "mm1", "cpv", "cps", "off5s", "yv", "ys", "yst", "qws", "sst", "sls", "p1",
+              "p2a", "p2b", "loc", "zzs", "bq", "stq", "dupq", "valq", "valo", "vald", "w2s", "rst_", "r1c", "r1s", "r2c",
+              "r2s"]
+
+
+def bits(m):
+    return bin(m).count("1")
+
+
+def mask_of(es):
+    return sum(1 << x for x in es)
 
 
 def plan(topo, ranks, r):
@@ -51,28 +59,56 @@ def plan(topo, ranks, r):
     order = [(r + i) % N for i in range(1, N)]
     far = [d for d in order if topo.chip(ranks[d]) != topo.chip(me)]
     near = [d for d in order if topo.chip(ranks[d]) == topo.chip(me)]
+    hands = [c for c in topo.cores_of(me) if c not in ranks and topo.die(c) == topo.die(me)]
     e = topo.engines(me, ranks[far[0]])
-
-    def m(es):
-        return sum(1 << x for x in es)
-    first = [(d, m(e[2 * i:2 * i + 2])) for i, d in enumerate(far[:4])]
-    second = [(d, m(e[4 * i:4 * i + 4])) for i, d in enumerate(far[4:])]
-    for d in near:
-        first.append((d, m([x for x in topo.engines(me, ranks[d]) if x not in e])))
-    return [first, second]
+    rest = [x for x in topo.engines(me, hands[0]) if x not in e]
+    direct = [(d, mask_of(e[2 * i:2 * i + 2])) for i, d in enumerate(far[:4])]
+    half = len(rest) // 2
+    via = [(d, hands[i], mask_of(rest[half * i:half * i + half]), topo.mask(hands[i], ranks[d]))
+           for i, d in enumerate(far[4:])]
+    return {"direct": direct, "via": via, "near": [(d, mask_of(rest)) for d in near]}
 
 
-def bits(m):
-    return bin(m).count("1")
+def dst_of(topo, c):
+    a = topo.addr(c)
+    return DstId(rid=a[0], pnc=a[1])
+
+
+def base(plans, s, d):
+    cyc = [(d + k) % N for k in range(1, N)]
+    late = [q for q in cyc if d in [v[0] for v in plans[q]["via"]]]
+    order = [q for q in cyc if q not in late] + late
+    return 0 if s == d else OWN + CAP * order.index(s)
+
+
+def hand_on(g, core, T, topo, ranks, plans):
+    for s in range(N):
+        for d, c, m_in, m_out in plans[s]["via"]:
+            if c != core:
+                continue
+            b = base(plans, s, d)
+            steps = [("rst_", T.relst[:], T.st[:, 8 * s:8 * s + 8], "sst"),
+                     ("r1c", T.rel1c[:].bitcast(dt.uint8), T.land1c[:, SW * s:SW * s + R1].bitcast(dt.uint8), "p1"),
+                     ("r1s", T.rel1s[:], T.land1s[:, SW * s:SW * s + R1], "p1"),
+                     ("r2c", T.rel2c[:].bitcast(dt.uint8), T.land2c[:, b:b + CAP].bitcast(dt.uint8), "p2b"),
+                     ("r2s", T.rel2s[:], T.land2s[:, b:b + CAP], "p2b")]
+            for sem, src, dst, rsem in steps:
+                g.wait_ge(T.sem[sem], bits(m_in))
+                g.remote_dma_fused([RemoteDMATransfer(dst_ids=[dst_of(topo, ranks[d])], dma_engine_mask=m_out,
+                                                      remote_sem=T.sem[rsem], src=src, dst=dst)], local_sem=T.sem.loc)
+            g.wait_ge(T.sem.loc, len(steps) * bits(m_out))
 
 
 def rank_program(g, core, T, topo):
     me = T.rank_of(core)
-    if me is None:
-        return
     ranks = list(T.cores)
+    plans = [plan(topo, ranks, r) for r in range(N)]
+    if me is None:
+        hand_on(g, core, T, topo, ranks, plans)
+        return
     V, S, Y, TE, sem = g.vector, g.scalar, g.sync, g.tensor, T.sem
     vn, ln = [0], [0]
+    mine = plans[me]
 
     def v(ins, name=None):
         if name is None:
@@ -96,153 +132,128 @@ def rank_program(g, core, T, topo):
     def scan(out, a, b, o0, o1, name=None):
         v(V.tensor_tensor_scan(out, a, b, 0.0, o0, o1), name)
 
-    def dst(d):
-        a = topo.addr(ranks[d])
-        return DstId(rid=a[0], pnc=a[1])
+    def fused(trs):
+        g.remote_dma_fused([RemoteDMATransfer(dst_ids=[dst_of(topo, c) for c in cs], dma_engine_mask=m, remote_sem=sem[rs],
+                                              srcs=[s], dsts=[d for c in cs]) for cs, m, rs, s, d in trs], local_sem=sem.loc)
+        ln[0] += sum(bits(t[1]) for t in trs)
 
-    def send(group, srcs, dsts, rsem):
-        ts_ = [RemoteDMATransfer(dst_ids=[dst(d)], dma_engine_mask=m, remote_sem=rsem, src=srcs(d), dst=dsts(d))
-               for d, m in group]
-        g.remote_dma_fused(ts_, local_sem=sem.loc)
-        ln[0] += sum(bits(m) for _, m in group)
+    def send_far(src, dst, rel, rsem, relsem):
+        fused([([ranks[d]], m, rsem, src(d), dst(d)) for d, m in mine["direct"]]
+              + [([c], m, relsem, src(d), rel) for d, c, m, mo in mine["via"]])
 
-    def tell(piece, rsem):
-        g.remote_dma_fused([RemoteDMATransfer(dst_ids=[dst(d) for d in everyone], dma_engine_mask=all_mask, remote_sem=rsem,
-                                              srcs=[piece], dsts=[piece for d in everyone])], local_sem=sem.loc)
-        ln[0] += bits(all_mask)
+    def send_near(src, dst, rsem):
+        fused([([ranks[d]], m, rsem, src(d), dst(d)) for d, m in mine["near"]])
 
-    plans = [plan(topo, ranks, r) for r in range(N)]
+    def incoming(kinds):
+        return sum(bits(t[-1]) for r in range(N) for k in kinds for t in plans[r][k] if t[0] == me)
+    every = ("direct", "near", "via")
 
-    def incoming(i):
-        return 2 * sum(bits(m) for r in range(N) if r != me for d, m in plans[r][i] if d == me)
-
-    def base(s, d):
-        order = [q for i in range(2) for k in range(1, N) for q in [(d + k) % N] if d in [x for x, _ in plans[q][i]]]
-        return 0 if s == d else OWN + CAP * order.index(s)
-
-    far_d = [d for d in range(N) if topo.chip(ranks[d]) != topo.chip(core)][0]
-    all_mask = topo.mask(core, ranks[far_d])
-    everyone = [(me + i) % N for i in range(1, N)]
-    nst = bits(all_mask) * (N - 1)
-    groups = plans[me]
+    all_mask = topo.mask(core, ranks[mine["direct"][0][0]])
+    nsl = bits(all_mask) * (N - 1)
 
     for q in range(8):
         (Y if q % 2 == 0 else S).dma_start(T.tab[16 * q:16 * q + 16, :], T.to[:]).then_inc(sem.lt, 16)
     S.dma_start(T.xt[:], T.x[:]).then_inc(sem.lx, 16)
-    Y.dma_start(T.wt[:], T.w[:]).then_inc(sem.lw, 16)
 
     def iota(out, pat, b, cm, s):
         g.iota(out, pat, b, cm, allow_small_or_imprecise_dtypes=True).then_inc(sem[s], 1)
     g.iota(T.pidx[:], [[0, 4]], 0, 1).then_inc(sem.gc1, 1)
-    iota(T.cc0[:], [[16, 24]], 0, 0, "gc1")
+    iota(T.torc[:], [[1, T0]], 0, 0, "gct")
     iota(T.k16[:], [[16, 4]], 0, 0, "gc2")
     iota(T.fl4[:], [[0, 2], [-32, 2]], 16, 0, "gc2")
     iota(T.cA[:], [[0, 8], [512, 8]], 7 - me, 0, "gc2")
     iota(T.cA2[:], [[-1, 8], [512, 8]], 7, 0, "gc2")
-    iota(T.dumpc[:], [[16, 32]], 2 * N * T0, 1, "gc2")
+    iota(T.d1[:, 1:64:2], [[16, 32]], N * T0, 1, "gc2")
 
     v(V.memset(T.zz[:], 0.0), "zzs")
-    v(V.memset(T.padr[:], float(PK - 1)), "wz")
-    v(V.memset(T.torow[:], 0.0), "wz")
-    v(V.memset(T.tabf[:], 0.0))
-    v(V.memset(T.tin[:], 0.0))
+    v(V.memset(T.padr[:], NOPL), "wz")
+    v(V.memset(T.W[:, 23:791:24], 0.0))
+    v(V.memset(T.tabk[:], 0.0))
     v(V.memset(T.z192[:], 0.0))
-    v(V.memset(T.rst[:], 1.0))
     v(V.memset(T.rst32[:], 1.0))
     v(V.memset(T.g1[:], 0))
     v(V.memset(T.ownl[:], 0))
-    V.wait_ge(sem.gc1, 2)
+    V.wait_ge(sem.gc1, 1)
     ts(T.pi15[:], T.pidx[:], 15, None, A.bitwise_and)
     ts(T.pi16[:], T.pidx[:], 16, None, A.bitwise_and)
     vw()
-    v(V.memset(T.rst[:, 0:192:24], 0.0))
     v(V.memset(T.rst32[:, 0:32:16], 0.0))
-    ts(T.par15[:], T.pi15[:, 0:1], 1.0, None, A.mult)
-    ts(T.par128[:], T.pi16[:, 0:1], 8.0, None, A.mult)
-    vw()
-    ts(T.cc[:], T.cc0[:], T.par15[:], float(PK), A.add, A.mult)
+    ts(T.par128[:], T.pi16[:, 0:1], 8.0, -1.0, A.mult, A.add)
+    ts(T.par1[:], T.pi16[:, 0:1], 0.0625, None, A.mult)
+    ts(T.epar[:], T.pi16[:, 0:1], -0.0625, 1.0, A.mult, A.add)
     v(V.memset(T.win1[:], 0.0))
-    vw()
     S.wait_ge(sem.zzs, 1)
-    for h in range(3):
+    for h in range(2):
         S.activation(T.srow[:, 768 * h:768 * h + 768], T.zz[:], AF.Copy).then_inc(sem.srz, 1)
 
+    vw()
     V.wait_ge(sem.lt, 128)
-    ts(T.key[:], T.tab[:], 1.0 / T0, 0.5 / T0 - 0.5, A.mult, A.add, "keyq")
-    ts(T.thi[:], T.tab[:], 0xFF0, None, A.bitwise_and)
-    tt(T.tabx[:], T.tab[:], T.cc[:], A.add)
+    cp(T.tabk[:, 0:24], T.tab[:], "gds")
+    ts(T.key[:], T.tab[:], 1.0 / T0, 0.5 / T0 - 0.5, A.mult, A.add, name="keyq")
+    V.wait_ge(sem.gds, 1)
+    v(V.transpose(T.trr[:], T.tabk[:]), "trs")
     V.wait_ge(sem.keyq, 1)
     for d in range(N):
-        if d == 3:
-            vw()
-            tt(T.tabf[:, 0:24], T.tabx[:], T.thi[:], A.add)
-        ts(T.M[:, 24 * d:24 * d + 24], T.key[:], float(d), None, A.is_equal, None, "ms")
-    vw()
-    v(V.transpose(T.trr[:], T.tabf[:]), "trs")
+        ts(T.M[:, 24 * d:24 * d + 24], T.key[:], float(d), None, A.is_equal, name="ms")
+    Y.wait_ge(sem.trs, 1)
+    Y.wait_ge(sem.gct, 1)
+    Y.dma_start(T.torc[1:2, :], T.trr[0:24, 0:16]).then_inc(sem.torw, 16)
+    Y.dma_start(T.wt[:], T.w[:]).then_inc(sem.lw, 16)
     V.wait_ge(sem.ms, N)
-    scan(T.W[:], T.M[:], T.z192[:], A.add, A.add)
+    scan(T.W[:, 24:216], T.M[:], T.z192[:], A.add, A.add)
+    S.wait_ge(sem.gds, 1)
+    for d in range(N):
+        S.activation(T.gd[:, d:192:8], T.tabk[:, 0:24], AF.Identity, 512.0 - 1024.0 * T0 * d, 1024.0).then_inc(sem.gds, 1)
     vw()
-    cp(T.tin[:, 1:9], T.W[:, 23:192:24])
-    vw()
-    v(V.transpose(T.tt0[:], T.tin[:]))
+    v(V.transpose(T.tt0[:], T.W[:, 23:791:24]))
     vw()
     scan(T.Qs[:], T.rst32[:], T.tt0[:], A.mult, A.add)
     vw()
+    ts(T.tb[:, 0:32], T.Qs[:], -1.0, T.Qs[:, 15:16], A.mult, A.add)
     tt(T.tb[:, 32:64], T.Qs[:], T.tt0[:], A.subtract)
+    vw()
+    v(V.transpose(T.tb2[:, 0:64], T.tb[:, 0:64]))
     ts(T.tb[:, 64:96], T.Qs[:], 0.0, T.Qs[:, 15:16], A.mult, A.add)
     vw()
-    ts(T.tb[:, 0:32], T.tb[:, 32:64], -1.0, T.Qs[:, 15:16], A.mult, A.add)
-    vw()
-    v(V.transpose(T.tb2[:], T.tb[:]))
+    tt(T.F[:], T.tb2[:, 0:8], T.tb2[:, 33:41], A.add, "fs")
+    v(V.transpose(T.tb2[:, 64:96], T.tb[:, 64:96]))
+    V.wait_ge(sem.fs, 1)
+    S.wait_ge(sem.fs, 1)
+    for d in range(5):
+        ts(T.td[:, d:192:8], T.W[:, 24 + 24 * d:48 + 24 * d], T.F[:, d:d + 1], None, A.add)
+    for d in range(5, N):
+        S.activation(T.td[:, d:192:8], T.W[:, 24 + 24 * d:48 + 24 * d], AF.Identity, T.F[:, d:d + 1]).then_inc(sem.tds, 1)
     vw()
     cp(T.st[:, 8 * me:8 * me + 8], T.tb2[:, 64:72], "sto")
-    tt(T.F[:], T.tb2[:, 0:8], T.tb2[:, 33:41], A.add)
-    S.wait_ge(sem.ms, N)
-    S.activation(T.M2[:], T.M[:], AF.Copy).then_inc(sem.m2, 1)
-    S.activation(T.Mm[:], T.M[:, 0:192:24], AF.Identity, -1.0).then_inc(sem.m2, 1)
-    V.wait_ge(sem.m2, 2)
+    V.wait_ge(sem.tds, N - 5)
+    V.wait_ge(sem.gds, N + 1)
+    scan(T.pos[:], T.gd[:], T.td[:], A.max, A.min)
     vw()
-    tt(T.M2[:, 0:192:24], T.Mm[:], T.F[:], A.add)
+    ts(T.off1[:], T.pos[:, 7:192:8], T.par128[:], None, A.add)
+    V.wait_ge(sem.gct, 1)
+    V.wait_ge(sem.torw, 16)
     vw()
-    scan(T.S[:], T.rst[:], T.M2[:], A.mult, A.add)
-    vw()
-    tt(T.Z[:], T.S[:], T.M[:], A.mult)
-    vw()
-    tt(T.Z1[:], T.Z[:, 0:96], T.Z[:, 96:192], A.add)
-    vw()
-    tt(T.Z2[:], T.Z1[:, 0:48], T.Z1[:, 48:96], A.add)
-    vw()
-    tt(T.P[:], T.Z2[:, 0:24], T.Z2[:, 24:48], A.add)
-    vw()
-    ts(T.u1[:], T.P[:], 384, None, A.bitwise_and)
-    vw()
-    tt(T.w1[:], T.P[:], T.u1[:], A.add)
-    vw()
-    ts(T.off1[:], T.w1[:], T.par128[:], None, A.add)
-    Y.wait_ge(sem.wz, 2)
-    Y.dma_start(T.sland[me, 96:128, :], T.padr[0:1, :]).then_inc(sem.stst, 16)
-    Y.wait_ge(sem.trs, 1)
-    for q in range(8):
-        Y.dma_start(T.torow[16 * q:16 * q + 1, :], T.trr[32 * (q // 2):32 * (q // 2) + 32, 0:16]).then_inc(sem.torw, 16)
-    V.wait_ge(sem.torw, 128)
-    V.wait_ge(sem.wz, 2)
-    vw()
-    cp(T.win1[:, 0:768].indirect(T.off1[:, 0:24]), T.torow[:, 0:T0], "scq")
+    cp(T.win1[:].indirect(T.off1[:, 0:24]), T.torc[:], "scq")
     V.wait_ge(sem.lx, 16)
     v(V.quantize_mx(T.qx[:], T.sx[:], T.xt[:]), "qxs")
     V.wait_ge(sem.scq, 1)
     for m in range(N):
-        v(V.transpose(T.tr1[:, 96 * m:96 * m + 96], T.win1[:, m:768:8]))
+        v(V.transpose(T.tr1[:, 64 * m:64 * m + 64], T.win1[:, m:512:8]))
     vw()
-    tt(T.G[:], T.tr1[:, 0:768:32], T.tr1[:, 16:768:32], A.add)
+    ts(T.Ge[:], T.tr1[:, 0:512:16], T.epar[:], None, A.mult)
+    ts(T.Go[:], T.tr1[:, 0:512:16], T.par1[:], None, A.mult)
     vw()
-    ts(T.gcol[:], T.G[:], 13, None, A.arith_shift_right)
+    tt(T.G[:, 0:24:3], T.Ge[:, 0:32:4], T.Go[:, 1:32:4], A.add)
+    tt(T.G[:, 1:24:3], T.Ge[:, 3:32:4], T.Go[:, 0:32:4], A.add)
+    tt(T.G[:, 2:24:3], T.Ge[:, 2:32:4], T.Go[:, 3:32:4], A.add)
     vw()
-    cp(T.g1[:, 0:24], T.gcol[:], "g1s")
-    cp(T.ownl[:, 0:3], T.gcol[:, 3 * me:3 * me + 3], "owns")
+    cp(T.g1[:, 0:24], T.G[:], "g1s")
+    cp(T.ownl[:, 0:3], T.G[:, 3 * me:3 * me + 3], "owns")
     V.wait_ge(sem.g1s, 1)
     V.wait_ge(sem.qxs, 1)
     cp(T.slot1c[:].bitcast(dt.uint32), T.qx[:].bitcast(dt.uint32).indirect(T.g1[:, 0:25]), "pk1c")
+    for h in range(2, 4):
+        S.activation(T.srow[:, 768 * h:768 * h + 768], T.zz[:], AF.Copy).then_inc(sem.srz, 1)
     S.wait_ge(sem.g1s, 1)
     S.wait_ge(sem.qxs, 1)
     S.activation(T.slot1s[:], T.sx[:].indirect(T.g1[:, 0:25]), AF.Copy).then_inc(sem.pk1s, 1)
@@ -251,35 +262,42 @@ def rank_program(g, core, T, topo):
     cp(T.land1c[:, own1].bitcast(dt.uint32), T.qx[:].bitcast(dt.uint32).indirect(T.ownl[:]), "own1c")
     S.wait_ge(sem.owns, 1)
     S.activation(T.land1s[:, own1], T.sx[:].indirect(T.ownl[:]), AF.Copy).then_inc(sem.own1s, 1)
+    for lo, hi in ((3072, 3840), (3840, 4096)):
+        S.activation(T.srow[:, lo:hi], T.zz[:, 0:hi - lo], AF.Copy).then_inc(sem.srz, 1)
+    Y.wait_ge(sem.wz, 1)
+    Y.dma_start(T.sland[me, 96:128, :], T.padr[0:1, :]).then_inc(sem.stst, 16)
     Y.wait_ge(sem.scq, 1)
-    for h in range(3):
-        Y.dma_start(T.sland[me, 32 * h:32 * h + 32, :], T.win1[0:1, 256 * h:256 * h + 128]).then_inc(sem.stst, 16)
+    Y.dma_start(T.sland[me, 0:96, :], T.win1[1:2, 0:T0]).then_inc(sem.stst, 16)
+    Y.wait_ge(sem.valq, N)
+    Y.wait_ge(sem.valo, N)
+    for q in range(4):
+        Y.dma_start(T.val[32 * q + 16:32 * q + 32, :], T.valo[32 * q + 16:32 * q + 32, :]).then_inc(sem.vald, 16)
 
-    g.wait_ge(sem.sto, 1)
-    tell(T.st[:, 8 * me:8 * me + 8], sem.sst)
-    land1 = slice(SW * me, SW * me + R1)
-
-    def codes1(grp):
-        send(grp, lambda d: T.slot1c[:, Q1 * d:Q1 * d + R1].bitcast(dt.uint8), lambda d: T.land1c[:, land1].bitcast(dt.uint8), sem.p1)
-
-    def scales1(grp):
-        send(grp, lambda d: T.slot1s[:, Q1 * d:Q1 * d + R1], lambda d: T.land1s[:, land1], sem.p1)
-    g.wait_ge(sem.pk1c, 1)
-    codes1(groups[0])
-    codes1(groups[1])
-    g.wait_ge(sem.stst, 64)
-    tell(T.sland[me], sem.sls)
-    g.wait_ge(sem.pk1s, 1)
-    scales1(groups[0])
-    scales1(groups[1])
     for m in range(N):
-        iota(T.val[:, SW * m:SW * m + SW], [[1, SW]], base(m, me) - 200, 0, "valq")
+        iota(T.val[:, SW * m:SW * m + SW], [[1, SW]], base(plans, m, me) - 200, 0, "valq")
+    g.wait_ge(sem.sto, 1)
+    mst = T.st[:, 8 * me:8 * me + 8]
+    fused([([ranks[d] for d, m in mine["direct"] + mine["near"]], all_mask, "sst", mst, mst)]
+          + [([c], m, "rst_", mst, T.relst[:]) for d, c, m, mo in mine["via"]])
+    land1 = slice(SW * me, SW * me + R1)
+    c1 = (lambda d: T.slot1c[:, Q1 * d:Q1 * d + R1].bitcast(dt.uint8), lambda d: T.land1c[:, land1].bitcast(dt.uint8))
+    s1 = (lambda d: T.slot1s[:, Q1 * d:Q1 * d + R1], lambda d: T.land1s[:, land1])
+    g.wait_ge(sem.pk1c, 1)
+    send_far(c1[0], c1[1], T.rel1c[:].bitcast(dt.uint8), "p1", "r1c")
+    g.wait_ge(sem.pk1s, 1)
+    send_far(s1[0], s1[1], T.rel1s[:], "p1", "r1s")
+    g.wait_ge(sem.stst, 32)
+    fused([([ranks[(me + i) % N] for i in range(1, N)], all_mask, "sls", T.sland[me], T.sland[me])])
+    send_near(c1[0], c1[1], "p1")
+    send_near(s1[0], s1[1], "p1")
+    for m in range(N):
+        iota(T.valo[:, SW * m:SW * m + SW], [[32, 2], [-16, 2], [1, 16]], base(plans, m, me) - 184, 0, "valo")
 
-    w2 = slice(2 * T0 * me, 2 * T0 * me + 2 * T0)
+    w2 = slice(T0 * me, T0 * me + T0 + 32)
     v(V.memset(T.stf[:, 64:72], float(T0)))
     v(V.memset(T.c8p[:], 0.0))
     v(V.memset(T.rst8[:], 1.0))
-    ts(T.par1[:], T.pi16[:, 0:1], 0.0625, None, A.mult)
+    v(V.memset(T.d0[:, 0:64:2], BIG))
     ts(T.par16[:], T.pi16[:, 0:1], 1.0, None, A.mult)
     V.wait_ge(sem.gc2, 5)
     tt(T.kp[:], T.pi15[:], T.k16[:], A.add)
@@ -296,7 +314,7 @@ def rank_program(g, core, T, topo):
     ts(T.kpo8[:], T.kpo[:], 8.0, None, A.mult)
     ts(T.nko8[:], T.kpo[:], -8.0, None, A.mult)
 
-    V.wait_ge(sem.sst, nst)
+    V.wait_ge(sem.sst, nsl)
     V.wait_ge(sem.sto, 1)
     for d in range(N):
         cp(T.stf[:, 8 * d:8 * d + 8], T.st[:, d:64:8], "stq")
@@ -327,8 +345,30 @@ def rank_program(g, core, T, topo):
     S.wait_ge(sem.bq, 1)
     for m in range(N):
         S.activation(T.nBx[:, 8 * m:8 * m + 8], T.nB[:, 8 * me:8 * me + 8], AF.Identity, float(m), 8.0).then_inc(sem.dupq, 1)
-    for lo, hi in ((2304, 3072), (3072, 3840), (3840, 4096)):
-        S.activation(T.srow[:, lo:hi], T.zz[:, 0:hi - lo], AF.Copy).then_inc(sem.srz, 1)
+
+    V.wait_ge(sem.off2s, 4)
+    V.wait_ge(sem.own1c, 1)
+    V.wait_ge(sem.p1, 2 * incoming(every))
+    cp(T.slot2c[:].bitcast(dt.uint32), T.land1c[:].bitcast(dt.uint32).indirect(T.off2[:]), "pk2c")
+    cp(T.land2c[:, 0:OWN].bitcast(dt.uint32), T.land1c[:].bitcast(dt.uint32).indirect(T.off2[:, 4 * me:4 * me + 4]), "own2c")
+    S.wait_ge(sem.off2s, 4)
+    S.wait_ge(sem.p1, 2 * incoming(every))
+    S.wait_ge(sem.own1s, 1)
+    S.activation(T.slot2s[:], T.land1s[:].indirect(T.off2[:]), AF.Copy).then_inc(sem.pk2s, 1)
+    S.activation(T.land2s[:, 0:OWN], T.land1s[:].indirect(T.off2[:, 4 * me:4 * me + 4]), AF.Copy).then_inc(sem.own2s, 1)
+
+    def blk(d):
+        b = base(plans, me, d)
+        return slice(b, b + CAP)
+    c2 = (lambda d: T.slot2c[:, SW * d:SW * d + CAP].bitcast(dt.uint8), lambda d: T.land2c[:, blk(d)].bitcast(dt.uint8))
+    s2 = (lambda d: T.slot2s[:, SW * d:SW * d + CAP], lambda d: T.land2s[:, blk(d)])
+    g.wait_ge(sem.pk2c, 1)
+    send_far(c2[0], c2[1], T.rel2c[:].bitcast(dt.uint8), "p2a", "r2c")
+    g.wait_ge(sem.pk2s, 1)
+    send_far(s2[0], s2[1], T.rel2s[:], "p2a", "r2s")
+    send_near(c2[0], c2[1], "p2a")
+    send_near(s2[0], s2[1], "p2a")
+
     V.wait_ge(sem.dupq, 2 * N)
     tt(T.ai2[:], T.stx[:], T.cA2[:], A.add)
     for kk in range(4):
@@ -343,32 +383,9 @@ def rank_program(g, core, T, topo):
     vw()
     for kk in range(4):
         ts(T.off3[:, kk:32:4], T.sc2[:, 64 * kk + 7:64 * kk + 64:8], T.kpo8[:, kk:kk + 1], 4095.0, A.add, A.min)
-
-    V.wait_ge(sem.off2s, 4)
-    V.wait_ge(sem.own1c, 1)
-    V.wait_ge(sem.p1, incoming(0) + incoming(1))
-    cp(T.slot2c[:].bitcast(dt.uint32), T.land1c[:].bitcast(dt.uint32).indirect(T.off2[:]), "pk2c")
-    cp(T.land2c[:, 0:OWN].bitcast(dt.uint32), T.land1c[:].bitcast(dt.uint32).indirect(T.off2[:, 4 * me:4 * me + 4]), "own2c")
-    S.wait_ge(sem.off2s, 4)
-    S.wait_ge(sem.p1, incoming(0) + incoming(1))
-    S.wait_ge(sem.own1s, 1)
-    S.activation(T.slot2s[:], T.land1s[:].indirect(T.off2[:]), AF.Copy).then_inc(sem.pk2s, 1)
-    S.activation(T.land2s[:, 0:OWN], T.land1s[:].indirect(T.off2[:, 4 * me:4 * me + 4]), AF.Copy).then_inc(sem.own2s, 1)
-
-    def blk(d):
-        return slice(base(me, d), base(me, d) + CAP)
-    g.wait_ge(sem.pk2c, 1)
-    for i, grp in enumerate(groups):
-        rs = sem["p2" + "ab"[i]]
-        send(grp, lambda d: T.slot2c[:, SW * d:SW * d + CAP].bitcast(dt.uint8),
-             lambda d: T.land2c[:, blk(d)].bitcast(dt.uint8), rs)
-        if i == 0:
-            g.wait_ge(sem.pk2s, 1)
-        send(grp, lambda d: T.slot2s[:, SW * d:SW * d + CAP], lambda d: T.land2s[:, blk(d)], rs)
-
     Y.wait_ge(sem.srz, 6)
-    Y.wait_ge(sem.stst, 64)
-    Y.wait_ge(sem.sls, nst)
+    Y.wait_ge(sem.stst, 32)
+    Y.wait_ge(sem.sls, nsl)
     for q in range(8):
         Y.dma_start(T.srow[16 * q:16 * q + 1, :], T.sland[:]).then_inc(sem.srl, 16)
     V.wait_ge(sem.srl, 128)
@@ -377,37 +394,32 @@ def rank_program(g, core, T, topo):
     vw()
     v(V.transpose(T.tr3[:], T.sg2[:]))
     vw()
-    tt(T.pd[:], T.tr3[:, 0:512:32], T.tr3[:, 16:512:32], A.subtract)
+    for h in range(2):
+        ts(T.d0[:, 2 * h + 1:64:4], T.tr3[:, 16 * h:512:32], float(T0 * me + T0), BIG, A.is_ge, A.mult)
+        cp(T.d1[:, 2 * h:64:4], T.tr3[:, 16 * h:512:32])
     vw()
-    ts(T.pe[:], T.pd[:], T.par1[:], None, A.mult)
+    scan(T.pl[:], T.d0[:], T.d1[:], A.max, A.min)
     vw()
-    tt(T.pt[:, 0:32:2], T.tr3[:, 0:512:32], T.pe[:], A.subtract)
-    tt(T.pt[:, 1:32:2], T.tr3[:, 16:512:32], T.pe[:], A.add)
-    vw()
-    ts(T.pq[:], T.pt[:], PK - 1, None, A.bitwise_and)
-    vw()
-    ts(T.pg[:], T.pq[:], float(2 * T0 * me + 2 * T0), BIG, A.is_ge, A.mult)
-    vw()
-    tt(T.pu[:], T.pq[:], T.pg[:], A.add)
-    vw()
-    tt(T.pl[:], T.pu[:], T.dumpc[:], A.min)
-    vw()
-    ts(T.off4[:], T.pl[:], T.par16[:], None, A.add)
+    ts(T.off4[:], T.pl[:, 1:64:2], T.par16[:], None, A.add)
     vw()
     V.wait_ge(sem.w2s, 1)
-    V.wait_ge(sem.valq, N)
+    V.wait_ge(sem.vald, 64)
     cp(T.win2[:].indirect(T.off4[:]), T.val[:])
     vw()
     v(V.transpose(T.tr2[:], T.win2[:, w2]))
     vw()
-    tt(T.G2[:], T.tr2[:, 0:768:32], T.tr2[:, 16:768:32], A.add)
+    ts(T.Ie[:], T.tr2[:, 0:416:16], T.epar[:], None, A.mult)
+    ts(T.Io[:], T.tr2[:, 0:416:16], T.par1[:], None, A.mult)
     vw()
-    ts(T.off5[:], T.G2[:], 200.0, None, A.add, None, "off5s")
+    tt(T.G2[:, 0:24:2], T.Ie[:, 0:24:2], T.Io[:, 1:24:2], A.add)
+    tt(T.G2[:, 1:24:2], T.Ie[:, 3:26:2], T.Io[:, 0:24:2], A.add)
+    vw()
+    ts(T.off5[:], T.G2[:], 200.0, None, A.add, name="off5s")
 
-    for s_, n_ in (("p2a", incoming(0)), ("own2c", 1), ("own2s", 1), ("qws", 1)):
+    for s_, n_ in (("p2a", 2 * incoming(("direct", "near"))), ("own2c", 1), ("own2s", 1), ("qws", 1)):
         TE.wait_ge(sem[s_], n_)
     TE.matmul_mx(T.ps[:, 0:L1], T.qw[:], T.sw[:], T.land2c[:, 0:L1], T.land2s[:, 0:L1], True, True).then_inc(sem.mm0, 1)
-    TE.wait_ge(sem.p2b, incoming(1))
+    TE.wait_ge(sem.p2b, 2 * incoming(("via",)))
     TE.matmul_mx(T.ps[:, 512:640], T.qw[:], T.sw[:], T.land2c[:, L2 - 128:L2], T.land2s[:, L2 - 128:L2], True, True).then_inc(sem.mm1, 1)
     S.wait_ge(sem.mm0, 1)
     S.activation(T.ysb[:, 0:L1], T.ps[:, 0:L1], AF.Copy).then_inc(sem.cps, 1)

from concourse.bass import DstId, RemoteDMATransfer
from concourse.mybir import dt, AluOpType as A, ActivationFunctionType as AF

T0, N, Q1, CAP, SW = 384, 8, 48, 56, 64
R1 = Q1 + 1
OWN = 64
L2 = OWN + 7 * CAP
L1 = L2 - 2 * CAP
NOPL = 8191.0
BIG = 65536.0
X4, U8, U16, F32, BF, I32 = "float8_e4m3fn_x4", "uint8", "uint16", "float32", "bfloat16", "int32"


def sb(n, t):
    return ("sbuf", [128, n], t)


SCRATCH = {
    "xt": sb(1536, BF), "wt": sb(512, BF), "qx": sb(T0, X4), "sx": sb(T0, U8), "qw": sb(128, X4), "sw": sb(128, U8),
    "slot1c": sb(400, X4), "slot1s": sb(400, U8), "land1c": sb(512, X4), "land1s": sb(512, U8),
    "slot2c": sb(512, X4), "slot2s": sb(512, U8), "land2c": sb(L2, X4), "land2s": sb(L2, U8),
    "relst": sb(8, U16), "rel1c": sb(R1, X4), "rel1s": sb(R1, U8), "rel2c": sb(CAP, X4), "rel2s": sb(CAP, U8),
    "tab": sb(24, I32), "key": sb(24, I32), "tabk": sb(32, F32), "M": sb(192, F32),
    "W": sb(816, F32), "z192": sb(192, F32), "rst32": sb(32, F32), "rst8": sb(64, F32),
    "gd": sb(192, F32), "td": sb(192, F32), "pos": sb(192, F32), "trr": sb(32, F32),
    "torc": sb(T0, F32), "padr": sb(128, F32), "tt0": sb(32, F32),
    "Qs": sb(32, F32), "tb": sb(96, F32), "tb2": sb(96, F32), "F": sb(8, F32), "off1": sb(24, U16),
    "win1": sb(512, F32), "tr1": sb(512, F32), "Ge": sb(32, F32), "Go": sb(32, F32), "G": sb(24, F32),
    "g1": sb(26, U16), "ownl": sb(4, U16), "srow": sb(4096, F32), "zz": sb(768, BF),
    "pidx": sb(4, I32), "pi15": sb(4, I32), "pi16": sb(4, I32), "par15": sb(1, F32), "par128": sb(1, F32),
    "par16": sb(1, F32), "par1": sb(1, F32), "epar": sb(1, F32), "k16": sb(4, F32), "fl4": sb(4, F32), "kp": sb(4, F32),
    "kt": sb(4, F32), "kpo": sb(4, F32), "kpo8": sb(4, F32), "nk": sb(4, F32), "nko8": sb(4, F32), "cA": sb(64, F32),
    "cA2": sb(64, F32), "st": sb(64, U16), "stf": sb(72, F32), "nn": sb(64, I32), "ai": sb(64, I32), "ci": sb(64, I32),
    "ti": sb(64, I32), "c8p": sb(66, F32), "nB": sb(64, F32), "ge": sb(256, F32), "tq": sb(64, F32), "sc": sb(256, F32),
    "off2": sb(32, U16), "nBx": sb(64, F32), "stx": sb(64, F32), "ai2": sb(64, I32), "ti2": sb(64, I32),
    "tq2": sb(64, F32), "ge2": sb(256, F32), "sc2": sb(256, F32), "off3": sb(32, U16),
    "sg2": sb(512, F32), "tr3": sb(512, F32), "d0": sb(64, F32), "d1": sb(64, F32), "pl": sb(64, F32), "off4": sb(32, U16),
    "val": sb(512, BF), "valo": sb(512, BF), "win2": sb(3712, BF), "tr2": sb(416, BF), "Ie": sb(26, F32),
    "Io": sb(26, F32), "G2": sb(24, F32), "off5": sb(24, U16), "ysb": sb(L2, F32), "yo": sb(T0, F32),
    "sland": ("dram", [8, 128, 4], F32), "ps": ("psum", [128, 1024], F32),
}
SEMAPHORES = ["vq", "gc1", "gct", "gc2", "lt", "lx", "lw", "keyq", "ms", "gds", "fs", "tds", "trs", "torw", "sto", "qxs",
              "g1s", "pk1c", "pk1s", "scq", "owns", "own1c", "own1s", "stst", "srz", "wz", "off2s", "pk2c", "pk2s",
              "own2c", "own2s", "srl", "mm0", "mm1", "cpv", "cps", "off5s", "yv", "ys", "yst", "qws", "sst", "sls", "p1",
              "p2a", "p2b", "loc", "zzs", "bq", "stq", "dupq", "valq", "valo", "vald", "w2s", "rst_", "r1c", "r1s", "r2c",
              "r2s"]


def bits(m):
    return bin(m).count("1")


def mask_of(es):
    return sum(1 << x for x in es)


def plan(topo, ranks, r):
    me = ranks[r]
    order = [(r + i) % N for i in range(1, N)]
    far = [d for d in order if topo.chip(ranks[d]) != topo.chip(me)]
    near = [d for d in order if topo.chip(ranks[d]) == topo.chip(me)]
    hands = [c for c in topo.cores_of(me) if c not in ranks and topo.die(c) == topo.die(me)]
    e = topo.engines(me, ranks[far[0]])
    rest = [x for x in topo.engines(me, hands[0]) if x not in e]
    direct = [(d, mask_of(e[2 * i:2 * i + 2])) for i, d in enumerate(far[:4])]
    half = len(rest) // 2
    via = [(d, hands[i], mask_of(rest[half * i:half * i + half]), topo.mask(hands[i], ranks[d]))
           for i, d in enumerate(far[4:])]
    return {"direct": direct, "via": via, "near": [(d, mask_of(rest)) for d in near]}


def dst_of(topo, c):
    a = topo.addr(c)
    return DstId(rid=a[0], pnc=a[1])


def base(plans, s, d):
    cyc = [(d + k) % N for k in range(1, N)]
    late = [q for q in cyc if d in [v[0] for v in plans[q]["via"]]]
    order = [q for q in cyc if q not in late] + late
    return 0 if s == d else OWN + CAP * order.index(s)


def hand_on(g, core, T, topo, ranks, plans):
    for s in range(N):
        for d, c, m_in, m_out in plans[s]["via"]:
            if c != core:
                continue
            b = base(plans, s, d)
            steps = [("rst_", T.relst[:], T.st[:, 8 * s:8 * s + 8], "sst"),
                     ("r1c", T.rel1c[:].bitcast(dt.uint8), T.land1c[:, SW * s:SW * s + R1].bitcast(dt.uint8), "p1"),
                     ("r1s", T.rel1s[:], T.land1s[:, SW * s:SW * s + R1], "p1"),
                     ("r2c", T.rel2c[:].bitcast(dt.uint8), T.land2c[:, b:b + CAP].bitcast(dt.uint8), "p2b"),
                     ("r2s", T.rel2s[:], T.land2s[:, b:b + CAP], "p2b")]
            for sem, src, dst, rsem in steps:
                g.wait_ge(T.sem[sem], bits(m_in))
                g.remote_dma_fused([RemoteDMATransfer(dst_ids=[dst_of(topo, ranks[d])], dma_engine_mask=m_out,
                                                      remote_sem=T.sem[rsem], src=src, dst=dst)], local_sem=T.sem.loc)
            g.wait_ge(T.sem.loc, len(steps) * bits(m_out))


def rank_program(g, core, T, topo):
    me = T.rank_of(core)
    ranks = list(T.cores)
    plans = [plan(topo, ranks, r) for r in range(N)]
    if me is None:
        hand_on(g, core, T, topo, ranks, plans)
        return
    V, S, Y, TE, sem = g.vector, g.scalar, g.sync, g.tensor, T.sem
    vn, ln = [0], [0]
    mine = plans[me]

    def v(ins, name=None):
        if name is None:
            ins.then_inc(sem.vq, 1)
            vn[0] += 1
        else:
            ins.then_inc(sem[name], 1)

    def vw():
        V.wait_ge(sem.vq, vn[0])

    def ts(out, in0, s1, s2, o0, o1=None, name=None):
        v(V.tensor_scalar(out, in0, s1, s2, o0, o1) if o1 is not None else V.tensor_scalar(out, in0, s1, s2, o0), name)

    def tt(out, a, b, op, name=None):
        v(V.tensor_tensor(out, a, b, op), name)

    def cp(out, in_, name=None):
        v(V.tensor_copy(out, in_), name)

    def scan(out, a, b, o0, o1, name=None):
        v(V.tensor_tensor_scan(out, a, b, 0.0, o0, o1), name)

    def fused(trs):
        g.remote_dma_fused([RemoteDMATransfer(dst_ids=[dst_of(topo, c) for c in cs], dma_engine_mask=m, remote_sem=sem[rs],
                                              srcs=[s], dsts=[d for c in cs]) for cs, m, rs, s, d in trs], local_sem=sem.loc)
        ln[0] += sum(bits(t[1]) for t in trs)

    def send_far(src, dst, rel, rsem, relsem):
        fused([([ranks[d]], m, rsem, src(d), dst(d)) for d, m in mine["direct"]]
              + [([c], m, relsem, src(d), rel) for d, c, m, mo in mine["via"]])

    def send_near(src, dst, rsem):
        fused([([ranks[d]], m, rsem, src(d), dst(d)) for d, m in mine["near"]])

    def incoming(kinds):
        return sum(bits(t[-1]) for r in range(N) for k in kinds for t in plans[r][k] if t[0] == me)
    every = ("direct", "near", "via")

    all_mask = topo.mask(core, ranks[mine["direct"][0][0]])
    nsl = bits(all_mask) * (N - 1)

    for q in range(8):
        (Y if q % 2 == 0 else S).dma_start(T.tab[16 * q:16 * q + 16, :], T.to[:]).then_inc(sem.lt, 16)
    S.dma_start(T.xt[:], T.x[:]).then_inc(sem.lx, 16)

    def iota(out, pat, b, cm, s):
        g.iota(out, pat, b, cm, allow_small_or_imprecise_dtypes=True).then_inc(sem[s], 1)
    g.iota(T.pidx[:], [[0, 4]], 0, 1).then_inc(sem.gc1, 1)
    iota(T.torc[:], [[1, T0]], 0, 0, "gct")
    iota(T.k16[:], [[16, 4]], 0, 0, "gc2")
    iota(T.fl4[:], [[0, 2], [-32, 2]], 16, 0, "gc2")
    iota(T.cA[:], [[0, 8], [512, 8]], 7 - me, 0, "gc2")
    iota(T.cA2[:], [[-1, 8], [512, 8]], 7, 0, "gc2")
    iota(T.d1[:, 1:64:2], [[16, 32]], N * T0, 1, "gc2")

    v(V.memset(T.zz[:], 0.0), "zzs")
    v(V.memset(T.padr[:], NOPL), "wz")
    v(V.memset(T.W[:, 23:791:24], 0.0))
    v(V.memset(T.tabk[:], 0.0))
    v(V.memset(T.z192[:], 0.0))
    v(V.memset(T.rst32[:], 1.0))
    v(V.memset(T.g1[:], 0))
    v(V.memset(T.ownl[:], 0))
    V.wait_ge(sem.gc1, 1)
    ts(T.pi15[:], T.pidx[:], 15, None, A.bitwise_and)
    ts(T.pi16[:], T.pidx[:], 16, None, A.bitwise_and)
    vw()
    v(V.memset(T.rst32[:, 0:32:16], 0.0))
    ts(T.par128[:], T.pi16[:, 0:1], 8.0, -1.0, A.mult, A.add)
    ts(T.par1[:], T.pi16[:, 0:1], 0.0625, None, A.mult)
    ts(T.epar[:], T.pi16[:, 0:1], -0.0625, 1.0, A.mult, A.add)
    v(V.memset(T.win1[:], 0.0))
    S.wait_ge(sem.zzs, 1)
    for h in range(2):
        S.activation(T.srow[:, 768 * h:768 * h + 768], T.zz[:], AF.Copy).then_inc(sem.srz, 1)

    vw()
    V.wait_ge(sem.lt, 128)
    cp(T.tabk[:, 0:24], T.tab[:], "gds")
    ts(T.key[:], T.tab[:], 1.0 / T0, 0.5 / T0 - 0.5, A.mult, A.add, name="keyq")
    V.wait_ge(sem.gds, 1)
    v(V.transpose(T.trr[:], T.tabk[:]), "trs")
    V.wait_ge(sem.keyq, 1)
    for d in range(N):
        ts(T.M[:, 24 * d:24 * d + 24], T.key[:], float(d), None, A.is_equal, name="ms")
    Y.wait_ge(sem.trs, 1)
    Y.wait_ge(sem.gct, 1)
    Y.dma_start(T.torc[1:2, :], T.trr[0:24, 0:16]).then_inc(sem.torw, 16)
    Y.dma_start(T.wt[:], T.w[:]).then_inc(sem.lw, 16)
    V.wait_ge(sem.ms, N)
    scan(T.W[:, 24:216], T.M[:], T.z192[:], A.add, A.add)
    S.wait_ge(sem.gds, 1)
    for d in range(N):
        S.activation(T.gd[:, d:192:8], T.tabk[:, 0:24], AF.Identity, 512.0 - 1024.0 * T0 * d, 1024.0).then_inc(sem.gds, 1)
    vw()
    v(V.transpose(T.tt0[:], T.W[:, 23:791:24]))
    vw()
    scan(T.Qs[:], T.rst32[:], T.tt0[:], A.mult, A.add)
    vw()
    ts(T.tb[:, 0:32], T.Qs[:], -1.0, T.Qs[:, 15:16], A.mult, A.add)
    tt(T.tb[:, 32:64], T.Qs[:], T.tt0[:], A.subtract)
    vw()
    v(V.transpose(T.tb2[:, 0:64], T.tb[:, 0:64]))
    ts(T.tb[:, 64:96], T.Qs[:], 0.0, T.Qs[:, 15:16], A.mult, A.add)
    vw()
    tt(T.F[:], T.tb2[:, 0:8], T.tb2[:, 33:41], A.add, "fs")
    v(V.transpose(T.tb2[:, 64:96], T.tb[:, 64:96]))
    V.wait_ge(sem.fs, 1)
    S.wait_ge(sem.fs, 1)
    for d in range(5):
        ts(T.td[:, d:192:8], T.W[:, 24 + 24 * d:48 + 24 * d], T.F[:, d:d + 1], None, A.add)
    for d in range(5, N):
        S.activation(T.td[:, d:192:8], T.W[:, 24 + 24 * d:48 + 24 * d], AF.Identity, T.F[:, d:d + 1]).then_inc(sem.tds, 1)
    vw()
    cp(T.st[:, 8 * me:8 * me + 8], T.tb2[:, 64:72], "sto")
    V.wait_ge(sem.tds, N - 5)
    V.wait_ge(sem.gds, N + 1)
    scan(T.pos[:], T.gd[:], T.td[:], A.max, A.min)
    vw()
    ts(T.off1[:], T.pos[:, 7:192:8], T.par128[:], None, A.add)
    V.wait_ge(sem.gct, 1)
    V.wait_ge(sem.torw, 16)
    vw()
    cp(T.win1[:].indirect(T.off1[:, 0:24]), T.torc[:], "scq")
    V.wait_ge(sem.lx, 16)
    v(V.quantize_mx(T.qx[:], T.sx[:], T.xt[:]), "qxs")
    V.wait_ge(sem.scq, 1)
    for m in range(N):
        v(V.transpose(T.tr1[:, 64 * m:64 * m + 64], T.win1[:, m:512:8]))
    vw()
    ts(T.Ge[:], T.tr1[:, 0:512:16], T.epar[:], None, A.mult)
    ts(T.Go[:], T.tr1[:, 0:512:16], T.par1[:], None, A.mult)
    vw()
    tt(T.G[:, 0:24:3], T.Ge[:, 0:32:4], T.Go[:, 1:32:4], A.add)
    tt(T.G[:, 1:24:3], T.Ge[:, 3:32:4], T.Go[:, 0:32:4], A.add)
    tt(T.G[:, 2:24:3], T.Ge[:, 2:32:4], T.Go[:, 3:32:4], A.add)
    vw()
    cp(T.g1[:, 0:24], T.G[:], "g1s")
    cp(T.ownl[:, 0:3], T.G[:, 3 * me:3 * me + 3], "owns")
    V.wait_ge(sem.g1s, 1)
    V.wait_ge(sem.qxs, 1)
    cp(T.slot1c[:].bitcast(dt.uint32), T.qx[:].bitcast(dt.uint32).indirect(T.g1[:, 0:25]), "pk1c")
    for h in range(2, 4):
        S.activation(T.srow[:, 768 * h:768 * h + 768], T.zz[:], AF.Copy).then_inc(sem.srz, 1)
    S.wait_ge(sem.g1s, 1)
    S.wait_ge(sem.qxs, 1)
    S.activation(T.slot1s[:], T.sx[:].indirect(T.g1[:, 0:25]), AF.Copy).then_inc(sem.pk1s, 1)
    V.wait_ge(sem.owns, 1)
    own1 = slice(SW * me, SW * me + SW)
    cp(T.land1c[:, own1].bitcast(dt.uint32), T.qx[:].bitcast(dt.uint32).indirect(T.ownl[:]), "own1c")
    S.wait_ge(sem.owns, 1)
    S.activation(T.land1s[:, own1], T.sx[:].indirect(T.ownl[:]), AF.Copy).then_inc(sem.own1s, 1)
    for lo, hi in ((3072, 3840), (3840, 4096)):
        S.activation(T.srow[:, lo:hi], T.zz[:, 0:hi - lo], AF.Copy).then_inc(sem.srz, 1)
    Y.wait_ge(sem.wz, 1)
    Y.dma_start(T.sland[me, 96:128, :], T.padr[0:1, :]).then_inc(sem.stst, 16)
    Y.wait_ge(sem.scq, 1)
    Y.dma_start(T.sland[me, 0:96, :], T.win1[1:2, 0:T0]).then_inc(sem.stst, 16)
    Y.wait_ge(sem.valq, N)
    Y.wait_ge(sem.valo, N)
    for q in range(4):
        Y.dma_start(T.val[32 * q + 16:32 * q + 32, :], T.valo[32 * q + 16:32 * q + 32, :]).then_inc(sem.vald, 16)

    for m in range(N):
        iota(T.val[:, SW * m:SW * m + SW], [[1, SW]], base(plans, m, me) - 200, 0, "valq")
    g.wait_ge(sem.sto, 1)
    mst = T.st[:, 8 * me:8 * me + 8]
    fused([([ranks[d] for d, m in mine["direct"] + mine["near"]], all_mask, "sst", mst, mst)]
          + [([c], m, "rst_", mst, T.relst[:]) for d, c, m, mo in mine["via"]])
    land1 = slice(SW * me, SW * me + R1)
    c1 = (lambda d: T.slot1c[:, Q1 * d:Q1 * d + R1].bitcast(dt.uint8), lambda d: T.land1c[:, land1].bitcast(dt.uint8))
    s1 = (lambda d: T.slot1s[:, Q1 * d:Q1 * d + R1], lambda d: T.land1s[:, land1])
    g.wait_ge(sem.pk1c, 1)
    send_far(c1[0], c1[1], T.rel1c[:].bitcast(dt.uint8), "p1", "r1c")
    g.wait_ge(sem.pk1s, 1)
    send_far(s1[0], s1[1], T.rel1s[:], "p1", "r1s")
    g.wait_ge(sem.stst, 32)
    fused([([ranks[(me + i) % N] for i in range(1, N)], all_mask, "sls", T.sland[me], T.sland[me])])
    send_near(c1[0], c1[1], "p1")
    send_near(s1[0], s1[1], "p1")
    for m in range(N):
        iota(T.valo[:, SW * m:SW * m + SW], [[32, 2], [-16, 2], [1, 16]], base(plans, m, me) - 184, 0, "valo")

    w2 = slice(T0 * me, T0 * me + T0 + 32)
    v(V.memset(T.stf[:, 64:72], float(T0)))
    v(V.memset(T.c8p[:], 0.0))
    v(V.memset(T.rst8[:], 1.0))
    v(V.memset(T.d0[:, 0:64:2], BIG))
    ts(T.par16[:], T.pi16[:, 0:1], 1.0, None, A.mult)
    V.wait_ge(sem.gc2, 5)
    tt(T.kp[:], T.pi15[:], T.k16[:], A.add)
    vw()
    v(V.memset(T.rst8[:, 0:64:8], 0.0))
    ts(T.kt[:], T.fl4[:], T.par1[:], None, A.mult)
    ts(T.nk[:], T.kp[:], -1.0, None, A.mult)
    v(V.memset(T.win2[:, w2], 0.0), "w2s")
    vw()
    tt(T.kpo[:], T.kp[:], T.kt[:], A.add)
    V.wait_ge(sem.lw, 16)
    v(V.quantize_mx(T.qw[:], T.sw[:], T.wt[:]), "qws")
    vw()
    ts(T.kpo8[:], T.kpo[:], 8.0, None, A.mult)
    ts(T.nko8[:], T.kpo[:], -8.0, None, A.mult)

    V.wait_ge(sem.sst, nsl)
    V.wait_ge(sem.sto, 1)
    for d in range(N):
        cp(T.stf[:, 8 * d:8 * d + 8], T.st[:, d:64:8], "stq")
    V.wait_ge(sem.stq, N)
    vw()
    tt(T.nn[:], T.stf[:, 0:64], T.stf[:, 8:72], A.subtract)
    tt(T.ai[:], T.stf[:, 0:64], T.cA[:], A.add)
    vw()
    ts(T.ci[:], T.nn[:], 3, None, A.arith_shift_right)
    ts(T.ti[:], T.ai[:], 3, None, A.arith_shift_right)
    vw()
    cp(T.c8p[:, 1:65], T.ci[:])
    vw()
    scan(T.nB[:], T.c8p[:, 0:64], T.rst8[:], A.add, A.mult, "bq")
    V.wait_ge(sem.bq, 1)
    tt(T.tq[:], T.ti[:], T.nB[:], A.add)
    for kk in range(4):
        ts(T.ge[:, 64 * kk:64 * kk + 64], T.nB[:], T.nk[:, kk:kk + 1], BIG, A.is_ge, A.mult)
    vw()
    for kk in range(4):
        scan(T.sc[:, 64 * kk:64 * kk + 64], T.ge[:, 64 * kk:64 * kk + 64], T.tq[:], A.max, A.min)
    vw()
    for kk in range(4):
        ts(T.off2[:, kk:32:4], T.sc[:, 64 * kk + 7:64 * kk + 64:8], T.kp[:, kk:kk + 1], float(7 * SW + Q1), A.add, A.min, "off2s")
    S.wait_ge(sem.stq, N)
    for m in range(N):
        S.activation(T.stx[:, 8 * m:8 * m + 8], T.stf[:, 8 * me:8 * me + 8], AF.Copy).then_inc(sem.dupq, 1)
    S.wait_ge(sem.bq, 1)
    for m in range(N):
        S.activation(T.nBx[:, 8 * m:8 * m + 8], T.nB[:, 8 * me:8 * me + 8], AF.Identity, float(m), 8.0).then_inc(sem.dupq, 1)

    V.wait_ge(sem.off2s, 4)
    V.wait_ge(sem.own1c, 1)
    V.wait_ge(sem.p1, 2 * incoming(every))
    cp(T.slot2c[:].bitcast(dt.uint32), T.land1c[:].bitcast(dt.uint32).indirect(T.off2[:]), "pk2c")
    cp(T.land2c[:, 0:OWN].bitcast(dt.uint32), T.land1c[:].bitcast(dt.uint32).indirect(T.off2[:, 4 * me:4 * me + 4]), "own2c")
    S.wait_ge(sem.off2s, 4)
    S.wait_ge(sem.p1, 2 * incoming(every))
    S.wait_ge(sem.own1s, 1)
    S.activation(T.slot2s[:], T.land1s[:].indirect(T.off2[:]), AF.Copy).then_inc(sem.pk2s, 1)
    S.activation(T.land2s[:, 0:OWN], T.land1s[:].indirect(T.off2[:, 4 * me:4 * me + 4]), AF.Copy).then_inc(sem.own2s, 1)

    def blk(d):
        b = base(plans, me, d)
        return slice(b, b + CAP)
    c2 = (lambda d: T.slot2c[:, SW * d:SW * d + CAP].bitcast(dt.uint8), lambda d: T.land2c[:, blk(d)].bitcast(dt.uint8))
    s2 = (lambda d: T.slot2s[:, SW * d:SW * d + CAP], lambda d: T.land2s[:, blk(d)])
    g.wait_ge(sem.pk2c, 1)
    send_far(c2[0], c2[1], T.rel2c[:].bitcast(dt.uint8), "p2a", "r2c")
    g.wait_ge(sem.pk2s, 1)
    send_far(s2[0], s2[1], T.rel2s[:], "p2a", "r2s")
    send_near(c2[0], c2[1], "p2a")
    send_near(s2[0], s2[1], "p2a")

    V.wait_ge(sem.dupq, 2 * N)
    tt(T.ai2[:], T.stx[:], T.cA2[:], A.add)
    for kk in range(4):
        ts(T.ge2[:, 64 * kk:64 * kk + 64], T.nBx[:], T.nko8[:, kk:kk + 1], BIG, A.is_ge, A.mult)
    vw()
    ts(T.ti2[:], T.ai2[:], 0xFFF8, None, A.bitwise_and)
    vw()
    tt(T.tq2[:], T.ti2[:], T.nBx[:], A.add)
    vw()
    for kk in range(4):
        scan(T.sc2[:, 64 * kk:64 * kk + 64], T.ge2[:, 64 * kk:64 * kk + 64], T.tq2[:], A.max, A.min)
    vw()
    for kk in range(4):
        ts(T.off3[:, kk:32:4], T.sc2[:, 64 * kk + 7:64 * kk + 64:8], T.kpo8[:, kk:kk + 1], 4095.0, A.add, A.min)
    Y.wait_ge(sem.srz, 6)
    Y.wait_ge(sem.stst, 32)
    Y.wait_ge(sem.sls, nsl)
    for q in range(8):
        Y.dma_start(T.srow[16 * q:16 * q + 1, :], T.sland[:]).then_inc(sem.srl, 16)
    V.wait_ge(sem.srl, 128)
    vw()
    cp(T.sg2[:], T.srow[:].indirect(T.off3[:]))
    vw()
    v(V.transpose(T.tr3[:], T.sg2[:]))
    vw()
    for h in range(2):
        ts(T.d0[:, 2 * h + 1:64:4], T.tr3[:, 16 * h:512:32], float(T0 * me + T0), BIG, A.is_ge, A.mult)
        cp(T.d1[:, 2 * h:64:4], T.tr3[:, 16 * h:512:32])
    vw()
    scan(T.pl[:], T.d0[:], T.d1[:], A.max, A.min)
    vw()
    ts(T.off4[:], T.pl[:, 1:64:2], T.par16[:], None, A.add)
    vw()
    V.wait_ge(sem.w2s, 1)
    V.wait_ge(sem.vald, 64)
    cp(T.win2[:].indirect(T.off4[:]), T.val[:])
    vw()
    v(V.transpose(T.tr2[:], T.win2[:, w2]))
    vw()
    ts(T.Ie[:], T.tr2[:, 0:416:16], T.epar[:], None, A.mult)
    ts(T.Io[:], T.tr2[:, 0:416:16], T.par1[:], None, A.mult)
    vw()
    tt(T.G2[:, 0:24:2], T.Ie[:, 0:24:2], T.Io[:, 1:24:2], A.add)
    tt(T.G2[:, 1:24:2], T.Ie[:, 3:26:2], T.Io[:, 0:24:2], A.add)
    vw()
    ts(T.off5[:], T.G2[:], 200.0, None, A.add, name="off5s")

    for s_, n_ in (("p2a", 2 * incoming(("direct", "near"))), ("own2c", 1), ("own2s", 1), ("qws", 1)):
        TE.wait_ge(sem[s_], n_)
    TE.matmul_mx(T.ps[:, 0:L1], T.qw[:], T.sw[:], T.land2c[:, 0:L1], T.land2s[:, 0:L1], True, True).then_inc(sem.mm0, 1)
    TE.wait_ge(sem.p2b, 2 * incoming(("via",)))
    TE.matmul_mx(T.ps[:, 512:640], T.qw[:], T.sw[:], T.land2c[:, L2 - 128:L2], T.land2s[:, L2 - 128:L2], True, True).then_inc(sem.mm1, 1)
    S.wait_ge(sem.mm0, 1)
    S.activation(T.ysb[:, 0:L1], T.ps[:, 0:L1], AF.Copy).then_inc(sem.cps, 1)
    V.wait_ge(sem.mm1, 1)
    cp(T.ysb[:, L1:L2], T.ps[:, 640 - L2 + L1:640], "cpv")
    for q in (V, S):
        q.wait_ge(sem.off5s, 1)
        q.wait_ge(sem.cpv, 1)
        q.wait_ge(sem.cps, 1)
    cp(T.yo[:, 0:192], T.ysb[:].indirect(T.off5[:, 0:12]), "yv")
    S.activation(T.yo[:, 192:384], T.ysb[:].indirect(T.off5[:, 12:24]), AF.Copy).then_inc(sem.ys, 1)
    Y.wait_ge(sem.yv, 1)
    Y.dma_start(T.y[:, 0:192], T.yo[:, 0:192]).then_inc(sem.yst, 16)
    S.wait_ge(sem.ys, 1)
    S.dma_start(T.y[:, 192:384], T.yo[:, 192:384]).then_inc(sem.yst, 16)
    Y.wait_ge(sem.yst, 32)
    g.wait_ge(sem.loc, ln[0])
